import numpy as np, ml_dtypes
CORES = [100,101,102,103,108,109,110,111]
N = 8
import mx_ref
NC, G, S2 = 128, 4, 1
C = np.float32(0.043)
CNT = [[0,0,4,24,20,0,12,68],[24,0,12,0,36,32,4,20],[24,12,0,36,0,8,48,0],[8,16,8,0,32,64,0,0],[0,20,80,4,0,16,8,0],[0,76,16,0,16,0,8,12],[72,0,0,8,12,8,0,28],[0,4,8,56,12,0,48,0]]
OFF = [[sum(c[:e]) for e in range(N + 1)] for c in CNT]
BF = ml_dtypes.bfloat16
def cut(t, i, w=512):
    return t[:, w * i:w * i + w]
def tile(rs):
    return np.stack(rs, axis=2).reshape(128, -1).astype(BF)
def layer(w, X):
    out = []
    for i in range(G):
        for t in range(len(X)):
            p = mx_ref.matmul(mx_ref.quantize(cut(w, len(X) * i + t)), X[t])
            z = p if t == 0 else z + p
        out.append(z)
    return out
def act(Z):
    return [np.maximum(z, 0) * C for z in Z]
def setup_inputs(rng):
    def f(*shape):
        return mx_ref.flush((rng.standard_normal(shape, dtype=np.float32) * np.exp2(rng.integers(-2, 3, shape[:-1] + (1,)))).astype(BF))
    gt = (0.125 + 0.875 * rng.random((N, 2, NC))).astype(BF)
    return {"gt": gt, "x": f(N, 128, 4 * NC), "w1": f(N, 128, G * 512), "w2": f(N, 128, 512)}
def setup_inputs_blocks(rng):
    d = setup_inputs(rng)
    for k in ("x", "w1", "w2"): d[k] = mx_ref.spread(d[k], rng, 4)
    return d
def setup_inputs_wide(rng):
    d = setup_inputs(rng)
    for k in ("x", "w1", "w2"): d[k] = mx_ref.flush((d[k].astype(np.float32) * np.exp2(rng.integers(-8, 9, (N, 1, 1))).astype(np.float32)).astype(BF))
    return d
def setup_inputs_zeros(rng):
    d = setup_inputs(rng); v = d["x"].reshape(N, 128, -1, 4).copy()
    v[np.broadcast_to((rng.random((N, 1, v.shape[2], 1)) < 0.33), v.shape)] = 0
    d["x"] = v.reshape(d["x"].shape)
    return d
def reference(gt, x, w1, w2):
    y = np.zeros((N, 128, NC), np.float32); g = gt.astype(np.float32)
    for e in range(N):
        f = (e - S2) % N
        t = np.concatenate([x[j][:, 4 * OFF[j][k]:4 * OFF[j][k + 1]] for k in (e, f) for j in range(N)], axis=1)
        p = mx_ref.matmul(mx_ref.quantize(w2[e]), mx_ref.quantize(tile(act(layer(w1[e], [mx_ref.quantize(t)])))))
        c = 0
        for i, k in enumerate((e, f)):
            for j in range(N):
                a, b = OFF[j][k], OFF[j][k + 1]
                y[j][:, a:b] = y[j][:, a:b] + p[:, c:c + b - a] * g[j, i, a:b]; c += b - a
    return {"y": y}

@@ -1,0 +1,450 @@
+from concourse.bass import DstId, RemoteDMATransfer
+from concourse.mybir import dt, AluOpType, ActivationFunctionType
+
+F8, U8, BF, F32 = "float8_e4m3fn_x4", "uint8", "bfloat16", "float32"
+C = 0.043
+NV = 80
+SCRATCH = {
+    "xt": ("sbuf", [128, 1024], BF),
+    "wt": ("sbuf", [128, 2560], BF),
+    "xq": ("sbuf", [128, 768], F8), "xs": ("sbuf", [128, 768], U8),
+    "wq": ("sbuf", [128, 640], F8), "ws": ("sbuf", [128, 640], U8),
+    "pq": ("sbuf", [128, 640], F8), "ps": ("sbuf", [128, 640], U8),
+    "cq1": ("sbuf", [128, 512], F8), "cs1": ("sbuf", [128, 512], U8),
+    "cq2": ("sbuf", [128, 512], F8), "cs2": ("sbuf", [128, 512], U8),
+    "gr": ("sbuf", [128, 256], BF), "gb": ("sbuf", [128, 256], BF),
+    "res0": ("sbuf", [128, 256], F32), "res1": ("sbuf", [128, 256], F32),
+    "ysb": ("sbuf", [128, 128], F32),
+    "z": ("psum", [128, 4096], F32),
+}
+for _i in range(3):
+    SCRATCH["h%d" % _i] = ("sbuf", [128, 1024], BF)
+    SCRATCH["hq%d" % _i] = ("sbuf", [128, 256], F8)
+    SCRATCH["hs%d" % _i] = ("sbuf", [128, 256], U8)
+    SCRATCH["po%d" % _i] = ("sbuf", [128, 256], F32)
+SEMAPHORES = ["lx", "lwa", "lwb", "lwc", "lg", "st", "rel", "xin", "g1", "g2", "wp", "pe", "pl0", "pl1", "ls"] + ["v%d" % i for i in range(NV)]
+
+
+def bits(mask):
+    return [i for i in range(32) if mask >> i & 1]
+
+
+def split(mask, k):
+    b = bits(mask)
+    n = len(b)
+    sizes = {1: [n], 2: [n // 2] * 2, 3: [n // 2, n // 4, n // 4], 4: [n // 4] * 4}[k]
+    out, a = [], 0
+    for s in sizes:
+        out.append(sum(1 << i for i in b[a:a + s]))
+        a += s
+    return out
+
+
+def make_plan(T, topo):
+    cores, cnt = T.cores, T.tables["CNT"]
+    n = len(cores)
+    P = {"n": n, "off": [[sum(c[:e]) for e in range(n + 1)] for c in cnt]}
+    grp = [[q for q in range(n) if topo.chip(cores[q]) == topo.chip(cores[r])] for r in range(n)]
+    far = [[q for q in range(n) if q not in grp[r]] for r in range(n)]
+    owner = [all(topo.may_write(cores[r], cores[q]) for q in far[r]) for r in range(n)]
+    ex = [[[q for q in grp[r] if owner[q] and q % 2 == p][0] for p in (0, 1)] for r in range(n)]
+
+    def run(e):
+        return [(e - 1) % n, e]
+
+    def size(j, segs):
+        return sum(cnt[j][s] for s in segs)
+
+    def farsegs(j, p):
+        return [s for e in far[j] if e % 2 == p for s in run(e)]
+
+    xo = [[(grp[r][0] - 1 + k) % n for k in range(n + 1)] for r in range(n)]
+
+    def locate(order, j, segs):
+        k = [i for i in range(len(order)) if order[i:i + len(segs)] == segs][0]
+        return size(j, order[:k])
+
+    tw = [size(r, xo[r]) for r in range(n)]
+
+    def window(j, dests):
+        dests = [(d, s) for d, s in dests if size(j, s)]
+        w = max([size(j, s) for d, s in dests] + [0])
+        out = []
+        for d, s in dests:
+            a = locate(xo[j], j, s)
+            st = min(a, tw[j] - w)
+            out.append((d, st, a - st))
+        return {"w": w, "to": out}
+
+    sends = []
+    for j in range(n):
+        rest = [q for q in grp[j] if q != j]
+        if owner[j]:
+            a = window(j, [(ex[far[j][0]][p], farsegs(j, p)) for p in (0, 1)])
+            b = window(j, [(q, run(q)) for q in rest])
+        else:
+            a = window(j, [(ex[j][p], run(ex[j][p]) + farsegs(j, p)) for p in (0, 1)])
+            b = window(j, [(q, run(q)) for q in rest if not owner[q]])
+        sends.append([a, b])
+
+    def incoming(r, j):
+        for g in sends[j]:
+            for i, (d, st, o) in enumerate(g["to"]):
+                if d == r:
+                    return g["w"], o, len(bits(split(topo.mask(cores[j], cores[r]), len(g["to"]))[i]))
+        return 0, 0, 0
+
+    lay = []
+    for r in range(n):
+        rest = [q for q in grp[r] if q != r]
+        if owner[r]:
+            non = [q for q in rest if not owner[q]]
+            best = None
+            for o in (non, non[::-1]):
+                L = {"fwd": None}
+                order = o + [q for q in rest if owner[q]]
+                tot = sum(incoming(r, q)[0] for q in order)
+                pos, at = -tot % 16, {}
+                for q in order:
+                    at[q] = pos + incoming(r, q)[1]
+                    pos += incoming(r, q)[0]
+                ends = []
+                for q in o:
+                    a = at[q] + size(q, run(r))
+                    ends.append((q, a, a + size(q, farsegs(q, r % 2))))
+                a, b = ends[0][1], ends[-1][2]
+                b = max(b, a + 128)
+                L = {"order": order, "at": at, "own": pos, "relay": o, "fwd": (a, b), "far": [(q, x - a) for q, x, y in ends]}
+                if best is None or b - a < best["fwd"][1] - best["fwd"][0]:
+                    best = L
+            lay.append(best)
+        else:
+            order = [q for q in rest if not owner[q]] + [q for q in rest if owner[q]]
+            pos, at = -sum(incoming(r, q)[0] for q in order) % 16, {}
+            for q in order:
+                at[q] = pos + incoming(r, q)[1]
+                pos += incoming(r, q)[0]
+            lay.append({"order": order, "at": at, "own": pos, "relay": []})
+        lay[r]["start"] = {}
+        for q in lay[r]["order"]:
+            lay[r]["start"][q] = lay[r]["at"][q] - incoming(r, q)[1]
+    ro = [[[(grp[r][0] - 1 + p + k) % n for k in range(n)] for p in (0, 1)] for r in range(n)]
+    P.update(cores=cores, cnt=cnt, grp=grp, far=far, owner=owner, ex=ex, run=run, size=size, farsegs=farsegs, xo=xo, tw=tw,
+             locate=locate, sends=sends, incoming=incoming, lay=lay, ro=ro)
+    return P
+
+
+def rank_program(g, core, T, topo):
+    me = T.rank_of(core)
+    if me is None:
+        return
+    P = make_plan(T, topo)
+    n, cores, cnt, grp, far, owner, ex = P["n"], P["cores"], P["cnt"], P["grp"], P["far"], P["owner"], P["ex"]
+    run, size, farsegs, locate, incoming = P["run"], P["size"], P["farsegs"], P["locate"], P["incoming"]
+    lay, off, par = P["lay"][me], P["off"], me % 2
+    S, V, A, M, Y = T.sem, g.vector, g.scalar, g.tensor, g.sync
+    count, local = [0], [0]
+
+    def ev():
+        count[0] += 1
+        return S["v%d" % (count[0] - 1)]
+
+    def dst(q):
+        a = topo.addr(cores[q])
+        return DstId(rid=a[0], pnc=a[1])
+
+    def mask(q):
+        return topo.mask(core, cores[q])
+
+    def copy(q, out, in_, sem):
+        a = topo.addr(cores[q])
+        g.remote_dma(out_ap=out, in_ap=in_, remote_sem=sem, local_sem=S["ls"], pid=a[1], routing_id=a[0], dma_engine_mask=mask(q))
+        local[0] += len(bits(mask(q)))
+
+    def fused(items):
+        if len(items) == 1:
+            return copy(*items[0])
+        ms = split(mask(items[0][0]), len(items))
+        g.remote_dma_fused([RemoteDMATransfer(dst_ids=[dst(q)], dma_engine_mask=m, remote_sem=sem, src=i, dst=o)
+                            for (q, o, i, sem), m in zip(items, ms)], local_sem=S["ls"])
+        local[0] += sum(len(bits(m)) for m in ms)
+
+    def codes(t, a, b):
+        return T[t][:, a:b].bitcast(dt.uint8)
+
+    order, base = P["xo"][me], grp[me][0]
+    tw, first = P["tw"][me], order[0]
+    if first == n - 1:
+        parts = [(Y, off[me][0], off[me][n], cnt[me][first]), (A, off[me][first], off[me][n], 0)]
+    else:
+        h = off[me][n] - off[me][first]
+        parts = [(Y, off[me][first], off[me][n], 0), (A, 0, off[me][first + 1], h)]
+    nx = 0
+    for q, a, b, c in parts:
+        if b > a:
+            q.dma_start(T.xt[:, 4 * c:4 * (c + b - a)], T.x[:, 4 * a:4 * b]).then_inc(S["lx"], 16)
+            nx += 16
+    Y.dma_start(T.wt[:, 0:1024], T.w1[:, 0:1024]).then_inc(S["lwa"], 16)
+    A.dma_start(T.wt[:, 1024:2048], T.w1[:, 1024:2048]).then_inc(S["lwb"], 16)
+    Y.dma_start(T.wt[:, 2048:2560], T.w2[:, :]).then_inc(S["lwc"], 16)
+    rpos = []
+    ng = 0
+    for p in (0, 1):
+        pos, c = {}, 0
+        for s in P["ro"][me][p]:
+            pos[s] = c
+            w = cnt[me][s]
+            if w:
+                i = 0 if s % 2 == p else 1
+                Y.dma_start(T.gr[0:1, 128 * p + c:128 * p + c + w], T.gt[i:i + 1, off[me][s]:off[me][s] + w]).then_inc(S["lg"], 16)
+                ng += 16
+            c += w
+        rpos.append(pos)
+
+    groups = []
+    pieces = []
+    for q in [q for q in grp[me] if q != me] + [me]:
+        w = size(q, run(me))
+        if w:
+            pieces.append((q, lay["own"] + locate(order, me, run(me)) if q == me else lay["at"][q], w, 0))
+    groups.append({"q": "xq", "s": "xs", "w": lay["own"] + tw, "pieces": pieces})
+    if owner[me]:
+        fl = P["ex"][far[me][0]]
+        duo = [e for e in grp[me] if e % 2 == par]
+        def far_group(at, buf, width):
+            qs = sorted(at, key=lambda q: size(q, farsegs(q, par)))
+            pc = []
+            for q in qs:
+                c = at[q]
+                for e in duo:
+                    w = size(q, run(e))
+                    if w:
+                        pc.append((q, c, w, 0 if e == me else 1))
+                    c += w
+            return {"q": "cq%d" % buf, "s": "cs%d" % buf, "w": width, "pieces": pc, "ranks": [q for q in qs if size(q, farsegs(q, par))]}
+        at, c = {}, 0
+        for q in fl:
+            w, o, k = incoming(me, q)
+            at[q] = c + o
+            c += w
+        groups.append(far_group(at, 1, c))
+        relay = fl[par]
+        rl = P["lay"][relay]
+        groups.append(far_group(dict(rl["far"]), 2, rl["fwd"][1] - rl["fwd"][0]))
+    for i, G in enumerate(groups):
+        c, hc = 0, []
+        for pc in G["pieces"]:
+            hc.append(c)
+            c += pc[2]
+        G["hc"], G["n"], G["nh"], G["i"] = hc, c, max(128, c), i
+
+    def span(G, slot):
+        cs = [(pc[1], pc[1] + pc[2]) for pc in G["pieces"] if pc[3] == slot]
+        lo, hi = min(a for a, b in cs), max(b for a, b in cs)
+        if hi - lo < 128:
+            lo = max(0, min(lo, G["w"] - 128))
+            hi = max(hi, lo + 128)
+        return lo, hi
+
+    pad = {}
+    for G in groups:
+        if G["n"] < 128:
+            pad[G["i"]] = ev()
+            V.memset(T["h%d" % G["i"]][:, 4 * G["n"]:512], 0.0).then_inc(pad[G["i"]], 1)
+    own = lay["own"]
+    V.wait_ge(S["lx"], nx)
+    qx, qw = ev(), ev()
+    V.quantize_mx(T.xq[:, own:own + tw], T.xs[:, own:own + tw], T.xt[:, 0:4 * tw]).then_inc(qx, 1)
+    for sem, a, b in (("lwa", 0, 256), ("lwb", 256, 512), ("lwc", 512, 640)):
+        V.wait_ge(S[sem], 16)
+        V.quantize_mx(T.wq[:, a:b], T.ws[:, a:b], T.wt[:, 4 * a:4 * b]).then_inc(qw, 1)
+
+    g.wait_ge(qx, 1)
+    for k, grpsend in enumerate(P["sends"][me]):
+        w = grpsend["w"]
+        cross = owner[me] and k == 0
+        for plane in (0, 1):
+            items = []
+            for q, st, o in grpsend["to"]:
+                if cross:
+                    at = 0 if par == 0 else incoming(q, P["ex"][me][0])[0]
+                    buf, sem = ("cs1", "cq1"), "g1"
+                else:
+                    at = P["lay"][q]["start"][me]
+                    buf, sem = ("xs", "xq"), "rel" if owner[q] and not owner[me] else "xin"
+                if plane:
+                    items.append((q, T[buf[0]][:, at:at + w], T.xs[:, own + st:own + st + w], S[sem]))
+                else:
+                    items.append((q, codes(buf[1], at, at + w), codes("xq", own + st, own + st + w), S[sem]))
+            if items:
+                fused(items)
+    nrel = sum(2 * incoming(me, q)[2] for q in lay["relay"])
+    nxin = sum(2 * incoming(me, q)[2] for q in lay["order"] if q not in lay["relay"])
+    if owner[me]:
+        a, b = lay["fwd"]
+        to = fl[par]
+        g.wait_ge(S["rel"], nrel)
+        g.wait_ge(qx, 1)
+        copy(to, codes("cq2", 0, b - a), codes("xq", a, b), S["g2"])
+        copy(to, T.cs2[:, 0:b - a], T.xs[:, a:b], S["g2"])
+    else:
+        to = ex[me][par]
+        g.wait_ge(qw, 3)
+        copy(to, codes("pq", 0, 640), codes("wq", 0, 640), S["wp"])
+        copy(to, T.ps[:, 0:640], T.ws[:, 0:640], S["wp"])
+    g.wait_ge(S["lg"], ng)
+    gb = ev()
+    g.partition_broadcast(T.gb[:, :], T.gr[0:1, :], 128).then_inc(gb, 1)
+
+    def bank(k, w):
+        return T.z[:, 512 * k:512 * k + w]
+
+    def product(k, wt, a, G, buf, lo, hi, sem):
+        M.matmul_mx(bank(k, hi - lo), T[wt[0]][:, a:a + 128], T[wt[1]][:, a:a + 128], T[buf[0]][:, lo:hi], T[buf[1]][:, lo:hi],
+                    True, True).then_inc(sem, 1)
+
+    weights = [("wq", "ws"), ("pq", "ps")]
+    M.wait_ge(qw, 3)
+    M.wait_ge(qx, 1)
+    if nrel:
+        M.wait_ge(S["rel"], nrel)
+    if nxin:
+        M.wait_ge(S["xin"], nxin)
+    zb = {(0, 0): [0, 1, 2, 3], (1, 0): [5, 6, 7, 0], (1, 1): [1, 2, 3, 4], (2, 0): [7, 0, 1, 2], (2, 1): [3, 4, 5, 6]}
+    pb = {(0, 0): 4, (1, 0): 5, (1, 1): 6, (2, 0): 7, (2, 1): 0}
+    done = {}
+    for G in groups:
+        i = G["i"]
+        h, slots = T["h%d" % i], sorted(set(pc[3] for pc in G["pieces"]))
+        if i:
+            M.wait_ge(S["g%d" % i], 2 * len(bits(topo.mask(cores[fl[par]], core))) if i == 2 else sum(2 * incoming(me, q)[2] for q in fl))
+        va, sa, nva, nsa = ev(), ev(), 0, 0
+        for slot in slots:
+            lo, hi = span(G, slot)
+            if i == 1 and slot == 1:
+                M.wait_ge(S["wp"], 2 * len(bits(topo.mask(cores[[q for q in duo if q != me][0]], core))))
+            for b in range(4):
+                k = zb[i, slot][b]
+                if (i, slot, b) == (1, 1, 3):
+                    M.wait_ge(done[0][0], done[0][1])
+                if (i, slot, b) == (2, 1, 2):
+                    for s, c in done[1]:
+                        M.wait_ge(s, c)
+                zs = ev()
+                product(k, weights[slot], 128 * b, G, (G["q"], G["s"]), lo, hi, zs)
+                E = V if b < 2 else A
+                E.wait_ge(zs, 1)
+                for pc, c in zip(G["pieces"], G["hc"]):
+                    if pc[3] != slot:
+                        continue
+                    src = T.z[:, 512 * k + pc[1] - lo:512 * k + pc[1] - lo + pc[2]]
+                    out = h[:, 4 * c + b:4 * (c + pc[2]):4]
+                    if b < 2:
+                        V.tensor_scalar(out, src, 0.0, C, AluOpType.max, AluOpType.mult).then_inc(va, 1)
+                        nva += 1
+                    else:
+                        A.activation(out, src, ActivationFunctionType.Relu, scale=C).then_inc(sa, 1)
+                        nsa += 1
+        V.wait_ge(va, nva)
+        V.wait_ge(sa, nsa)
+        if i in pad:
+            V.wait_ge(pad[i], 1)
+        qh = ev()
+        V.quantize_mx(T["hq%d" % i][:, 0:G["nh"]], T["hs%d" % i][:, 0:G["nh"]], h[:, 0:4 * G["nh"]]).then_inc(qh, 1)
+        M.wait_ge(qh, 1)
+        po = T["po%d" % i]
+        done[i] = []
+        for slot in slots:
+            pz = ev()
+            product(pb[i, slot], weights[slot], 512, G, ("hq%d" % i, "hs%d" % i), 0, G["nh"], pz)
+            ce, nce = ev(), 0
+            E = A if i == 0 or slot == 1 else V
+            E.wait_ge(pz, 1)
+            jobs = []
+            if i == 0:
+                m = sum(pc[2] for pc in G["pieces"] if pc[0] != me)
+                if m:
+                    jobs.append((po[:, 0:m], 0, m))
+                if size(me, run(me)):
+                    r0 = rpos[par][run(me)[0]]
+                    jobs.append((T["res%d" % par][:, r0:r0 + G["n"] - m], m, G["n"]))
+            else:
+                jobs = [(po[:, c:c + pc[2]], c, c + pc[2]) for pc, c in zip(G["pieces"], G["hc"]) if pc[3] == slot]
+            for out, a, b in jobs:
+                src = T.z[:, 512 * pb[i, slot] + a:512 * pb[i, slot] + b]
+                if E is A:
+                    A.activation(out, src, ActivationFunctionType.Copy).then_inc(ce, 1)
+                else:
+                    V.tensor_copy(out, src).then_inc(ce, 1)
+                nce += 1
+            done[i].append((ce, nce))
+        if i == 0:
+            done[0] = done[0][0]
+
+        if i == 0:
+            g.wait_ge(done[0][0], done[0][1])
+            for pc, c in zip(G["pieces"], G["hc"]):
+                q = pc[0]
+                if q != me:
+                    a = locate(P["ro"][q][par], q, run(me))
+                    copy(q, T["res%d" % par][:, a:a + pc[2]], po[:, c:c + pc[2]], S["pe"])
+        else:
+            for s, c in done[i]:
+                g.wait_ge(s, c)
+            w = max(size(q, farsegs(q, par)) for q in G["ranks"])
+            c, items = 0, []
+            for q in G["ranks"]:
+                a = locate(P["ro"][q][par], q, farsegs(q, par))
+                items.append((q, T["res%d" % par][:, a:a + w], po[:, c:c + w], S["pl%d" % par]))
+                c += size(q, farsegs(q, par))
+            fused(items)
+
+    npe = sum(len(bits(topo.mask(cores[q], core))) for q in grp[me] if q != me and size(me, run(q)))
+    V.wait_ge(gb, 1)
+    V.wait_ge(done[0][0], done[0][1])
+    if npe:
+        V.wait_ge(S["pe"], npe)
+    me_s, nms = ev(), 0
+    early = [size(me, P["ro"][me][p][:4]) for p in (0, 1)]
+
+    def gate(p, a, b):
+        r = T["res%d" % p][:, a:b]
+        V.tensor_tensor(r, r, T.gb[:, 128 * p + a:128 * p + b], AluOpType.mult).then_inc(me_s, 1)
+
+    for p in (0, 1):
+        if early[p]:
+            gate(p, 0, early[p])
+            nms += 1
+    V.wait_ge(me_s, nms)
+    adds = []
+    for s in range(n):
+        w = cnt[me][s]
+        if not w:
+            continue
+        late = any(P["ro"][me][p].index(s) >= 4 for p in (0, 1))
+        a0, a1, y0 = rpos[0][s], rpos[1][s], off[me][s]
+        if adds and adds[-1][0] == late and adds[-1][1] + adds[-1][4] == a0 and adds[-1][2] + adds[-1][4] == a1:
+            adds[-1][4] += w
+        else:
+            adds.append([late, a0, a1, y0, w])
+    ys = ev()
+
+    def add(late):
+        for l, a0, a1, y0, w in adds:
+            if l == late:
+                V.tensor_tensor(T.ysb[:, y0:y0 + w], T.res0[:, a0:a0 + w], T.res1[:, a1:a1 + w], AluOpType.add).then_inc(ys, 1)
+
+    add(False)
+    for p in (0, 1):
+        if early[p] < 128:
+            e = ex[far[me][0]][p]
+            mates = [q for q in grp[me] if owner[q] == owner[me] and size(q, farsegs(q, p))]
+            V.wait_ge(S["pl%d" % p], len(bits(split(topo.mask(cores[e], core), len(mates))[0])))
+            gate(p, early[p], 128)
+            nms += 1
+    V.wait_ge(me_s, nms)
+    add(True)
+    Y.wait_ge(ys, len(adds))
+    Y.dma_start(T.y[:, :], T.ysb[:, :]).then_inc(S["st"], 16)
+    Y.wait_ge(S["st"], 16)
+    g.wait_ge(S["ls"], local[0])

@@ -4,33 +4,43 @@ from concourse.mybir import dt, AluOpType, ActivationFunctionType
 F8, U8, BF, F32 = "float8_e4m3fn_x4", "uint8", "bfloat16", "float32"
 C = 0.043
 NV = 80
+NSIM = 112
 SCRATCH = {
     "xt": ("sbuf", [128, 1024], BF),
     "wt": ("sbuf", [128, 2560], BF),
     "xq": ("sbuf", [128, 768], F8), "xs": ("sbuf", [128, 768], U8),
     "wq": ("sbuf", [128, 640], F8), "ws": ("sbuf", [128, 640], U8),
     "pq": ("sbuf", [128, 640], F8), "ps": ("sbuf", [128, 640], U8),
+    "rq": ("sbuf", [128, 512], F8), "rs": ("sbuf", [128, 512], U8),
     "cq1": ("sbuf", [128, 512], F8), "cs1": ("sbuf", [128, 512], U8),
     "cq2": ("sbuf", [128, 512], F8), "cs2": ("sbuf", [128, 512], U8),
+    "gd": ("dram", [128, 2], BF),
     "gr": ("sbuf", [128, 256], BF), "gb": ("sbuf", [128, 256], BF),
     "res0": ("sbuf", [128, 256], F32), "res1": ("sbuf", [128, 256], F32),
+    "po0": ("sbuf", [128, 512], F32),
+    "po1": ("sbuf", [128, 256], F32), "po2": ("sbuf", [128, 256], F32),
     "ysb": ("sbuf", [128, 128], F32),
     "z": ("psum", [128, 4096], F32),
 }
-for _i in range(3):
-    SCRATCH["h%d" % _i] = ("sbuf", [128, 1024], BF)
-    SCRATCH["hq%d" % _i] = ("sbuf", [128, 256], F8)
-    SCRATCH["hs%d" % _i] = ("sbuf", [128, 256], U8)
-    SCRATCH["po%d" % _i] = ("sbuf", [128, 256], F32)
-SEMAPHORES = ["lx", "lwa", "lwb", "lwc", "lg", "st", "rel", "xin", "g1", "g2", "wp", "pe", "pl0", "pl1", "ls"] + ["v%d" % i for i in range(NV)]
+for _i in range(4):
+    SCRATCH["ge%d" % _i] = ("dram", [128, 2], BF)
+for _i in (1, 2):
+    SCRATCH["gr%d" % _i] = ("sbuf", [128, 256], BF)
+    SCRATCH["gb%d" % _i] = ("sbuf", [128, 256], BF)
+for _i in ("0", "10", "11", "20", "21"):
+    SCRATCH["h" + _i] = ("sbuf", [128, 2048], BF)
+    SCRATCH["hq" + _i] = ("sbuf", [128, 512], F8)
+    SCRATCH["hs" + _i] = ("sbuf", [128, 512], U8)
+SEMAPHORES = ["lx", "lwa", "lwb", "lwc", "lg", "lgd", "lg1", "lg2", "ga", "gh", "st", "relc", "relp", "xin", "g1", "g2", "wp",
+              "pe", "pl0", "pl1", "ls"] + ["v%d" % i for i in range(NV)]
 
 
 def bits(mask):
     return [i for i in range(32) if mask >> i & 1]
 
 
-def split(mask, k):
-    b = bits(mask)
+def split(mask, k, last=0):
+    b = bits(mask & ~last) + bits(mask & last)
     n = len(b)
     sizes = {1: [n], 2: [n // 2] * 2, 3: [n // 2, n // 4, n // 4], 4: [n // 4] * 4}[k]
     out, a = [], 0
@@ -48,6 +58,8 @@ def make_plan(T, topo):
     far = [[q for q in range(n) if q not in grp[r]] for r in range(n)]
     owner = [all(topo.may_write(cores[r], cores[q]) for q in far[r]) for r in range(n)]
     ex = [[[q for q in grp[r] if owner[q] and q % 2 == p][0] for p in (0, 1)] for r in range(n)]
+    hp = [[c for c in range(NSIM) if c not in cores and topo.chip(c) == topo.chip(cores[r]) and
+           all(topo.may_write(c, cores[q]) for q in far[r])][:2] for r in range(n)]
 
     def run(e):
         return [(e - 1) % n, e]
@@ -58,7 +70,7 @@ def make_plan(T, topo):
     def farsegs(j, p):
         return [s for e in far[j] if e % 2 == p for s in run(e)]
 
-    xo = [[(grp[r][0] - 1 + k) % n for k in range(n + 1)] for r in range(n)]
+    xo = [[(r + k) % n for k in range(n + 1)] for r in range(n)]
 
     def locate(order, j, segs):
         k = [i for i in range(len(order)) if order[i:i + len(segs)] == segs][0]
@@ -67,81 +79,72 @@ def make_plan(T, topo):
     tw = [size(r, xo[r]) for r in range(n)]
 
     def window(j, dests):
-        dests = [(d, s) for d, s in dests if size(j, s)]
-        w = max([size(j, s) for d, s in dests] + [0])
+        dests = [(d, s, l) for d, s, l in dests if size(j, s)]
+        w = max([size(j, s) for d, s, l in dests] + [0])
         out = []
-        for d, s in dests:
-            a = locate(xo[j], j, s)
-            st = min(a, tw[j] - w)
+        for d, s, l in dests:
+            a, m = locate(xo[j], j, s), size(j, s)
+            st = max(0, a + m - w) if l else min(a, tw[j] - w)
             out.append((d, st, a - st))
         return {"w": w, "to": out}
 
     sends = []
     for j in range(n):
         rest = [q for q in grp[j] if q != j]
+        non = [q for q in grp[j] if not owner[q]]
         if owner[j]:
-            a = window(j, [(ex[far[j][0]][p], farsegs(j, p)) for p in (0, 1)])
-            b = window(j, [(q, run(q)) for q in rest])
+            a = window(j, [(cores[ex[far[j][0]][p]], farsegs(j, p), False) for p in (0, 1)])
         else:
-            a = window(j, [(ex[j][p], run(ex[j][p]) + farsegs(j, p)) for p in (0, 1)])
-            b = window(j, [(q, run(q)) for q in rest if not owner[q]])
+            a = window(j, [(hp[j][p], farsegs(j, p), j == non[0]) for p in (0, 1)])
+        b = window(j, [(cores[q], run(q), False) for q in [q for q in rest if owner[q]] + [q for q in rest if not owner[q]]])
         sends.append([a, b])
 
-    def incoming(r, j):
-        for g in sends[j]:
-            for i, (d, st, o) in enumerate(g["to"]):
-                if d == r:
-                    return g["w"], o, len(bits(split(topo.mask(cores[j], cores[r]), len(g["to"]))[i]))
-        return 0, 0, 0
+    def place(c, srcs, k, pos):
+        start, at = {}, {}
+        for q in srcs:
+            for d, st, o in sends[q][k]["to"]:
+                if d == c:
+                    start[q], at[q] = pos, pos + o
+                    pos += sends[q][k]["w"]
+        return start, at, pos
 
-    lay = []
+    near = []
     for r in range(n):
-        rest = [q for q in grp[r] if q != r]
-        if owner[r]:
-            non = [q for q in rest if not owner[q]]
-            best = None
-            for o in (non, non[::-1]):
-                L = {"fwd": None}
-                order = o + [q for q in rest if owner[q]]
-                tot = sum(incoming(r, q)[0] for q in order)
-                pos, at = -tot % 16, {}
-                for q in order:
-                    at[q] = pos + incoming(r, q)[1]
-                    pos += incoming(r, q)[0]
-                ends = []
-                for q in o:
-                    a = at[q] + size(q, run(r))
-                    ends.append((q, a, a + size(q, farsegs(q, r % 2))))
-                a, b = ends[0][1], ends[-1][2]
-                b = max(b, a + 128)
-                L = {"order": order, "at": at, "own": pos, "relay": o, "fwd": (a, b), "far": [(q, x - a) for q, x, y in ends]}
-                if best is None or b - a < best["fwd"][1] - best["fwd"][0]:
-                    best = L
-            lay.append(best)
-        else:
-            order = [q for q in rest if not owner[q]] + [q for q in rest if owner[q]]
-            pos, at = -sum(incoming(r, q)[0] for q in order) % 16, {}
-            for q in order:
-                at[q] = pos + incoming(r, q)[1]
-                pos += incoming(r, q)[0]
-            lay.append({"order": order, "at": at, "own": pos, "relay": []})
-        lay[r]["start"] = {}
-        for q in lay[r]["order"]:
-            lay[r]["start"][q] = lay[r]["at"][q] - incoming(r, q)[1]
+        own = -tw[r] % 16
+        start, at, end = place(cores[r], [q for q in grp[r] if q != r], 1, own + tw[r])
+        near.append({"own": own, "start": start, "at": at, "end": end})
+    direct, passed, relay = {}, {}, {}
+    for r in range(n):
+        if r != grp[r][0]:
+            continue
+        f = far[r]
+        for p in (0, 1):
+            c, rc = cores[ex[r][p]], hp[f[0]][p]
+            start, at, end = place(c, [q for q in f if owner[q]], 0, 0)
+            direct[c] = {"start": start, "at": at, "w": end}
+            start, at, end = place(rc, [q for q in f if not owner[q]], 0, 0)
+            a = min(at[q] for q in at)
+            b = max(at[q] + size(q, farsegs(q, p)) for q in at)
+            if b - a < 128:
+                b = min(end, a + 128)
+                a = b - 128
+            relay[rc] = {"start": start, "fwd": (a, b), "to": c}
+            passed[c] = {"at": {q: at[q] - a for q in at}, "w": b - a, "relay": rc}
+            for D in (direct[c], passed[c]):
+                D["ranks"] = sorted(D["at"], key=lambda q: size(q, farsegs(q, p)))
     ro = [[[(grp[r][0] - 1 + p + k) % n for k in range(n)] for p in (0, 1)] for r in range(n)]
-    P.update(cores=cores, cnt=cnt, grp=grp, far=far, owner=owner, ex=ex, run=run, size=size, farsegs=farsegs, xo=xo, tw=tw,
-             locate=locate, sends=sends, incoming=incoming, lay=lay, ro=ro)
+    P.update(cores=cores, cnt=cnt, grp=grp, far=far, owner=owner, ex=ex, hp=hp, run=run, size=size, farsegs=farsegs, xo=xo, tw=tw,
+             locate=locate, sends=sends, near=near, direct=direct, passed=passed, relay=relay, ro=ro)
     return P
 
 
 def rank_program(g, core, T, topo):
-    me = T.rank_of(core)
-    if me is None:
-        return
     P = make_plan(T, topo)
-    n, cores, cnt, grp, far, owner, ex = P["n"], P["cores"], P["cnt"], P["grp"], P["far"], P["owner"], P["ex"]
-    run, size, farsegs, locate, incoming = P["run"], P["size"], P["farsegs"], P["locate"], P["incoming"]
-    lay, off, par = P["lay"][me], P["off"], me % 2
+    n, cores, cnt, grp, far, owner, ex, hp = P["n"], P["cores"], P["cnt"], P["grp"], P["far"], P["owner"], P["ex"], P["hp"]
+    run, size, farsegs, locate, off = P["run"], P["size"], P["farsegs"], P["locate"], P["off"]
+    me = T.rank_of(core)
+    if me is None and core not in P["relay"]:
+        return
     S, V, A, M, Y = T.sem, g.vector, g.scalar, g.tensor, g.sync
     count, local = [0], [0]
 
@@ -149,94 +152,89 @@ def rank_program(g, core, T, topo):
         count[0] += 1
         return S["v%d" % (count[0] - 1)]
 
-    def dst(q):
-        a = topo.addr(cores[q])
-        return DstId(rid=a[0], pnc=a[1])
+    def engines(s, d):
+        return len(bits(topo.mask(s, d)))
 
-    def mask(q):
-        return topo.mask(core, cores[q])
+    def off_chip(s, d):
+        r = T.rank_of(s)
+        return topo.mask(s, cores[far[r][0]]) if r is not None and owner[r] and topo.chip(s) == topo.chip(d) else 0
 
-    def copy(q, out, in_, sem):
-        a = topo.addr(cores[q])
-        g.remote_dma(out_ap=out, in_ap=in_, remote_sem=sem, local_sem=S["ls"], pid=a[1], routing_id=a[0], dma_engine_mask=mask(q))
-        local[0] += len(bits(mask(q)))
+    def copy(c, out, in_, sem):
+        a = topo.addr(c)
+        g.remote_dma(out_ap=out, in_ap=in_, remote_sem=sem, local_sem=S["ls"], pid=a[1], routing_id=a[0], dma_engine_mask=topo.mask(core, c))
+        local[0] += engines(core, c)
 
     def fused(items):
         if len(items) == 1:
             return copy(*items[0])
-        ms = split(mask(items[0][0]), len(items))
-        g.remote_dma_fused([RemoteDMATransfer(dst_ids=[dst(q)], dma_engine_mask=m, remote_sem=sem, src=i, dst=o)
-                            for (q, o, i, sem), m in zip(items, ms)], local_sem=S["ls"])
+        ms = split(topo.mask(core, items[0][0]), len(items), off_chip(core, items[0][0]))
+        ts = []
+        for (c, o, i, sem), m in zip(items, ms):
+            a = topo.addr(c)
+            ts.append(RemoteDMATransfer(dst_ids=[DstId(rid=a[0], pnc=a[1])], dma_engine_mask=m, remote_sem=sem, src=i, dst=o))
+        g.remote_dma_fused(ts, local_sem=S["ls"])
         local[0] += sum(len(bits(m)) for m in ms)
+
+    def share(c, s, to):
+        ms = split(topo.mask(s, to[0]), len(to), off_chip(s, to[0])) if to else []
+        return sum(len(bits(m)) for d, m in zip(to, ms) if d == c)
+
+    def arrive(c, j, k):
+        return share(c, cores[j], [t[0] for t in P["sends"][j][k]["to"]])
+
+    def gdest(r):
+        return [cores[q] for q in ex[far[r][0]]] if owner[r] else hp[r]
 
     def codes(t, a, b):
         return T[t][:, a:b].bitcast(dt.uint8)
 
-    order, base = P["xo"][me], grp[me][0]
-    tw, first = P["tw"][me], order[0]
-    if first == n - 1:
-        parts = [(Y, off[me][0], off[me][n], cnt[me][first]), (A, off[me][first], off[me][n], 0)]
-    else:
-        h = off[me][n] - off[me][first]
-        parts = [(Y, off[me][first], off[me][n], 0), (A, 0, off[me][first + 1], h)]
-    nx = 0
-    for q, a, b, c in parts:
-        if b > a:
-            q.dma_start(T.xt[:, 4 * c:4 * (c + b - a)], T.x[:, 4 * a:4 * b]).then_inc(S["lx"], 16)
-            nx += 16
-    Y.dma_start(T.wt[:, 0:1024], T.w1[:, 0:1024]).then_inc(S["lwa"], 16)
-    A.dma_start(T.wt[:, 1024:2048], T.w1[:, 1024:2048]).then_inc(S["lwb"], 16)
-    Y.dma_start(T.wt[:, 2048:2560], T.w2[:, :]).then_inc(S["lwc"], 16)
-    rpos = []
-    ng = 0
-    for p in (0, 1):
-        pos, c = {}, 0
-        for s in P["ro"][me][p]:
-            pos[s] = c
-            w = cnt[me][s]
-            if w:
-                i = 0 if s % 2 == p else 1
-                Y.dma_start(T.gr[0:1, 128 * p + c:128 * p + c + w], T.gt[i:i + 1, off[me][s]:off[me][s] + w]).then_inc(S["lg"], 16)
-                ng += 16
-            c += w
-        rpos.append(pos)
+    if me is None:
+        R = P["relay"][core]
+        a, b = R["fwd"]
+        home = [r for r in range(n) if topo.chip(cores[r]) == topo.chip(core)]
+        src = [q for q in home if not owner[q]]
+        g.wait_ge(S["ga"], sum(share(core, cores[q], gdest(q)) for q in src))
+        fused([(R["to"], T["ge%d" % home.index(q)][:, :], T["ge%d" % home.index(q)][:, :], S["gh"]) for q in src])
+        nrel = sum(arrive(core, q, 0) for q in R["start"])
+        g.wait_ge(S["relc"], nrel)
+        copy(R["to"], codes("cq2", 0, b - a), codes("rq", a, b), S["g2"])
+        g.wait_ge(S["relp"], nrel)
+        copy(R["to"], T.cs2[:, 0:b - a], T.rs[:, a:b], S["g2"])
+        g.wait_ge(S["ls"], local[0])
+        return
 
-    groups = []
+    par, faro = me % 2, far[me]
+    weights = [("wq", "ws"), ("pq", "ps")]
+
+    lay = P["near"][me]
+    own, tw = lay["own"], P["tw"][me]
     pieces = []
     for q in [q for q in grp[me] if q != me] + [me]:
         w = size(q, run(me))
         if w:
-            pieces.append((q, lay["own"] + locate(order, me, run(me)) if q == me else lay["at"][q], w, 0))
-    groups.append({"q": "xq", "s": "xs", "w": lay["own"] + tw, "pieces": pieces})
-    if owner[me]:
-        fl = P["ex"][far[me][0]]
-        duo = [e for e in grp[me] if e % 2 == par]
-        def far_group(at, buf, width):
-            qs = sorted(at, key=lambda q: size(q, farsegs(q, par)))
-            pc = []
-            for q in qs:
-                c = at[q]
-                for e in duo:
-                    w = size(q, run(e))
-                    if w:
-                        pc.append((q, c, w, 0 if e == me else 1))
-                    c += w
-            return {"q": "cq%d" % buf, "s": "cs%d" % buf, "w": width, "pieces": pc, "ranks": [q for q in qs if size(q, farsegs(q, par))]}
-        at, c = {}, 0
-        for q in fl:
-            w, o, k = incoming(me, q)
-            at[q] = c + o
-            c += w
-        groups.append(far_group(at, 1, c))
-        relay = fl[par]
-        rl = P["lay"][relay]
-        groups.append(far_group(dict(rl["far"]), 2, rl["fwd"][1] - rl["fwd"][0]))
-    for i, G in enumerate(groups):
-        c, hc = 0, []
+            pieces.append((q, own + locate(P["xo"][me], me, run(me)) if q == me else lay["at"][q], w, 0))
+    groups = [{"q": "xq", "s": "xs", "w": lay["end"], "pieces": pieces, "i": 0}]
+    duo = [e for e in grp[me] if e % 2 == par]
+    partner = [e for e in duo if e != me][0]
+    for i, D in enumerate([P["direct"][core], P["passed"][core]] if owner[me] else []):
+        pieces = []
+        for q in D["ranks"]:
+            c = D["at"][q]
+            for e in duo:
+                w = size(q, run(e))
+                if w:
+                    pieces.append((q, c, w, 0 if e == me else 1))
+                c += w
+        groups.append({"q": "cq%d" % (i + 1), "s": "cs%d" % (i + 1), "w": D["w"], "pieces": pieces, "ranks": D["ranks"], "i": i + 1})
+    for G in groups:
+        c, ht, hc, rc = 0, {}, [], []
         for pc in G["pieces"]:
-            hc.append(c)
+            hc.append(ht.get(pc[3], 0))
+            ht[pc[3]] = hc[-1] + pc[2]
+            rc.append(c)
             c += pc[2]
-        G["hc"], G["n"], G["nh"], G["i"] = hc, c, max(128, c), i
+        G["hc"], G["rc"], G["n"], G["ht"] = hc, rc, c, ht
+        G["name"] = {sl: "0" if G["i"] == 0 else "%d%d" % (G["i"], sl) for sl in ht}
 
     def span(G, slot):
         cs = [(pc[1], pc[1] + pc[2]) for pc in G["pieces"] if pc[3] == slot]
@@ -247,11 +245,42 @@ def rank_program(g, core, T, topo):
         return lo, hi
 
     pad = {}
-    for G in groups:
-        if G["n"] < 128:
-            pad[G["i"]] = ev()
-            V.memset(T["h%d" % G["i"]][:, 4 * G["n"]:512], 0.0).then_inc(pad[G["i"]], 1)
-    own = lay["own"]
+    for G in groups[1:]:
+        for sl in sorted(G["ht"]):
+            if G["ht"][sl] < 128:
+                pad[G["i"], sl] = ev()
+                V.memset(T["h" + G["name"][sl]][:, 4 * G["ht"][sl]:512], 0.0).then_inc(pad[G["i"], sl], 1)
+
+    A.dma_start(T.gd[:, :], T.gt[:, :]).then_inc(S["lgd"], 16)
+    nx = 0
+    for q, a, b, c in [(Y, off[me][me], off[me][n], 0), (A, 0, off[me][me + 1], off[me][n] - off[me][me])]:
+        if b > a:
+            q.dma_start(T.xt[:, 4 * c:4 * (c + b - a)], T.x[:, 4 * a:4 * b]).then_inc(S["lx"], 16)
+            nx += 16
+    rpos, gates, gpos = [], [], [0]
+    for p in (0, 1):
+        pos, c = {}, 0
+        for k, s in enumerate(P["ro"][me][p]):
+            pos[s] = c
+            w = cnt[me][s]
+            if w and k < 4:
+                gates.append((gpos[p] + c, 0 if s % 2 == p else 1, off[me][s], w))
+            c += w
+        rpos.append(pos)
+        gpos.append(gpos[p] + size(me, P["ro"][me][p][:4]))
+    ng = 16 * len(gates)
+
+    def gate_loads(q, some):
+        for c, i, a, w in some:
+            q.dma_start(T.gr[0:1, c:c + w], T.gt[i:i + 1, a:a + w]).then_inc(S["lg"], 16)
+
+    few = 0 if off[me][me + 1] else 3
+    gate_loads(A, gates[:few])
+    Y.dma_start(T.wt[:, 0:1024], T.w1[:, 0:1024]).then_inc(S["lwa"], 16)
+    A.dma_start(T.wt[:, 1024:2048], T.w1[:, 1024:2048]).then_inc(S["lwb"], 16)
+    Y.dma_start(T.wt[:, 2048:2560], T.w2[:, :]).then_inc(S["lwc"], 16)
+    gate_loads(Y, gates[few:])
+
     V.wait_ge(S["lx"], nx)
     qx, qw = ev(), ev()
     V.quantize_mx(T.xq[:, own:own + tw], T.xs[:, own:own + tw], T.xt[:, 0:4 * tw]).then_inc(qx, 1)
@@ -259,163 +288,195 @@ def rank_program(g, core, T, topo):
         V.wait_ge(S[sem], 16)
         V.quantize_mx(T.wq[:, a:b], T.ws[:, a:b], T.wt[:, 4 * a:4 * b]).then_inc(qw, 1)
 
+    g.wait_ge(S["lgd"], 16)
+    slot_g = "ge%d" % grp[me].index(me)
+    fused([(c, T[slot_g][:, :], T.gd[:, :], S["ga"]) for c in gdest(me)])
     g.wait_ge(qx, 1)
-    for k, grpsend in enumerate(P["sends"][me]):
-        w = grpsend["w"]
-        cross = owner[me] and k == 0
+    for k, send in enumerate(P["sends"][me]):
+        w = send["w"]
         for plane in (0, 1):
             items = []
-            for q, st, o in grpsend["to"]:
-                if cross:
-                    at = 0 if par == 0 else incoming(q, P["ex"][me][0])[0]
-                    buf, sem = ("cs1", "cq1"), "g1"
+            for c, st, o in send["to"]:
+                if k == 1:
+                    at, buf, sem = P["near"][cores.index(c)]["start"][me], ("xs", "xq"), "xin"
+                elif owner[me]:
+                    at, buf, sem = P["direct"][c]["start"][me], ("cs1", "cq1"), "g1"
                 else:
-                    at = P["lay"][q]["start"][me]
-                    buf, sem = ("xs", "xq"), "rel" if owner[q] and not owner[me] else "xin"
+                    at, buf, sem = P["relay"][c]["start"][me], ("rs", "rq"), ("relp" if plane else "relc")
                 if plane:
-                    items.append((q, T[buf[0]][:, at:at + w], T.xs[:, own + st:own + st + w], S[sem]))
+                    items.append((c, T[buf[0]][:, at:at + w], T.xs[:, own + st:own + st + w], S[sem]))
                 else:
-                    items.append((q, codes(buf[1], at, at + w), codes("xq", own + st, own + st + w), S[sem]))
+                    items.append((c, codes(buf[1], at, at + w), codes("xq", own + st, own + st + w), S[sem]))
             if items:
                 fused(items)
-    nrel = sum(2 * incoming(me, q)[2] for q in lay["relay"])
-    nxin = sum(2 * incoming(me, q)[2] for q in lay["order"] if q not in lay["relay"])
-    if owner[me]:
-        a, b = lay["fwd"]
-        to = fl[par]
-        g.wait_ge(S["rel"], nrel)
-        g.wait_ge(qx, 1)
-        copy(to, codes("cq2", 0, b - a), codes("xq", a, b), S["g2"])
-        copy(to, T.cs2[:, 0:b - a], T.xs[:, a:b], S["g2"])
-    else:
-        to = ex[me][par]
+    if not owner[me]:
         g.wait_ge(qw, 3)
-        copy(to, codes("pq", 0, 640), codes("wq", 0, 640), S["wp"])
-        copy(to, T.ps[:, 0:640], T.ws[:, 0:640], S["wp"])
-    g.wait_ge(S["lg"], ng)
+        c = cores[ex[me][par]]
+        copy(c, codes("pq", 0, 640), codes("wq", 0, 640), S["wp"])
+        copy(c, T.ps[:, 0:640], T.ws[:, 0:640], S["wp"])
     gb = ev()
-    g.partition_broadcast(T.gb[:, :], T.gr[0:1, :], 128).then_inc(gb, 1)
+    if ng:
+        g.wait_ge(S["lg"], ng)
+        g.partition_broadcast(T.gb[:, 0:gpos[2]], T.gr[0:1, 0:gpos[2]], 128).then_inc(gb, 1)
+    gbx, ngx = {}, {}
+    for G in groups[1:]:
+        i, nl = G["i"], 0
+        if i == 1:
+            Y.wait_ge(S["ga"], sum(share(core, cores[q], gdest(q)) for q in faro if owner[q]))
+        else:
+            Y.wait_ge(S["gh"], engines(P["passed"][core]["relay"], core))
+        for (q, c, w, sl), r in zip(G["pieces"], G["rc"]):
+            e = me if sl == 0 else partner
+            for k, s in ((1, (e - 1) % n), (0, e)):
+                m, src = cnt[q][s], T["ge%d" % faro.index(q)]
+                if m:
+                    a = (k * 128 + off[q][s]) // 2
+                    Y.dma_start(T["gr%d" % i][0:1, r:r + m], src[a:a + m // 2, :]).then_inc(S["lg%d" % i], 16)
+                    nl += 16
+                r += m
+        gbx[i], ngx[i] = ev(), nl
 
-    def bank(k, w):
-        return T.z[:, 512 * k:512 * k + w]
+    def spread(i):
+        g.wait_ge(S["lg%d" % i], ngx[i])
+        g.partition_broadcast(T["gb%d" % i][:, 0:groups[i]["n"]], T["gr%d" % i][0:1, 0:groups[i]["n"]], 128).then_inc(gbx[i], 1)
 
-    def product(k, wt, a, G, buf, lo, hi, sem):
-        M.matmul_mx(bank(k, hi - lo), T[wt[0]][:, a:a + 128], T[wt[1]][:, a:a + 128], T[buf[0]][:, lo:hi], T[buf[1]][:, lo:hi],
-                    True, True).then_inc(sem, 1)
+    if owner[me]:
+        spread(1)
 
-    weights = [("wq", "ws"), ("pq", "ps")]
     M.wait_ge(qw, 3)
     M.wait_ge(qx, 1)
-    if nrel:
-        M.wait_ge(S["rel"], nrel)
+    nxin = sum(2 * arrive(core, q, 1) for q in grp[me] if q != me)
     if nxin:
         M.wait_ge(S["xin"], nxin)
-    zb = {(0, 0): [0, 1, 2, 3], (1, 0): [5, 6, 7, 0], (1, 1): [1, 2, 3, 4], (2, 0): [7, 0, 1, 2], (2, 1): [3, 4, 5, 6]}
-    pb = {(0, 0): 4, (1, 0): 5, (1, 1): 6, (2, 0): 7, (2, 1): 0}
-    done = {}
-    for G in groups:
-        i = G["i"]
-        h, slots = T["h%d" % i], sorted(set(pc[3] for pc in G["pieces"]))
+    units = [(G, sl) for G in groups for sl in sorted(G["ht"], key=lambda sl: -G["ht"][sl] if G["i"] == 2 else sl)]
+    acts, qhs, copied = {}, {}, {}
+
+    def product(bank, wt, a, buf, lo, hi, sem):
+        M.matmul_mx(T.z[:, 512 * bank:512 * bank + hi - lo], T[wt[0]][:, a:a + 128], T[wt[1]][:, a:a + 128],
+                    T[buf[0]][:, lo:hi], T[buf[1]][:, lo:hi], True, True).then_inc(sem, 1)
+
+    def width(k):
+        G, slot = units[k]
+        return max(128, G["ht"][slot]) if G["i"] else span(G, 0)[1] - span(G, 0)[0]
+
+    def make(k, between):
+        G, slot = units[k]
+        i, h = G["i"], T["h" + G["name"][slot]]
+        lo, hi = span(G, slot)
+        if i == 1 and units[k - 1][0] is not G:
+            M.wait_ge(S["g1"], sum(2 * arrive(core, q, 0) for q in faro if owner[q]))
+        if i == 2 and units[k - 1][0] is not G:
+            M.wait_ge(S["g2"], 2 * engines(P["passed"][core]["relay"], core))
+        if i == 1 and slot == 1:
+            M.wait_ge(S["wp"], 2 * engines(cores[partner], core))
         if i:
-            M.wait_ge(S["g%d" % i], 2 * len(bits(topo.mask(cores[fl[par]], core))) if i == 2 else sum(2 * incoming(me, q)[2] for q in fl))
+            todo = [(pc[1] - lo, pc[2], c) for pc, c in zip(G["pieces"], G["hc"]) if pc[3] == slot]
+        else:
+            todo = [(0, hi - lo, 0)]
         va, sa, nva, nsa = ev(), ev(), 0, 0
-        for slot in slots:
-            lo, hi = span(G, slot)
-            if i == 1 and slot == 1:
-                M.wait_ge(S["wp"], 2 * len(bits(topo.mask(cores[[q for q in duo if q != me][0]], core))))
-            for b in range(4):
-                k = zb[i, slot][b]
-                if (i, slot, b) == (1, 1, 3):
-                    M.wait_ge(done[0][0], done[0][1])
-                if (i, slot, b) == (2, 1, 2):
-                    for s, c in done[1]:
-                        M.wait_ge(s, c)
-                zs = ev()
-                product(k, weights[slot], 128 * b, G, (G["q"], G["s"]), lo, hi, zs)
-                E = V if b < 2 else A
-                E.wait_ge(zs, 1)
-                for pc, c in zip(G["pieces"], G["hc"]):
-                    if pc[3] != slot:
-                        continue
-                    src = T.z[:, 512 * k + pc[1] - lo:512 * k + pc[1] - lo + pc[2]]
-                    out = h[:, 4 * c + b:4 * (c + pc[2]):4]
-                    if b < 2:
-                        V.tensor_scalar(out, src, 0.0, C, AluOpType.max, AluOpType.mult).then_inc(va, 1)
-                        nva += 1
-                    else:
-                        A.activation(out, src, ActivationFunctionType.Relu, scale=C).then_inc(sa, 1)
-                        nsa += 1
+        for b in (0, 2, 1, 3):
+            bank = 4 * (k % 2) + b
+            if b == 3 and k > 1:
+                M.wait_ge(*copied[k - 2])
+            zs = ev()
+            product(bank, weights[slot], 128 * b, (G["q"], G["s"]), lo, hi, zs)
+            E = V if b < 2 else A
+            E.wait_ge(zs, 1)
+            for a, w, c in todo:
+                src = T.z[:, 512 * bank + a:512 * bank + a + w]
+                out = h[:, 4 * c + b:4 * (c + w):4]
+                if b < 2:
+                    V.tensor_scalar(out, src, 0.0, C, AluOpType.max, AluOpType.mult).then_inc(va, 1)
+                    nva += 1
+                else:
+                    A.activation(out, src, ActivationFunctionType.Relu, scale=C).then_inc(sa, 1)
+                    nsa += 1
+            if b == 0 and between is not None:
+                quantise(between)
+        acts[k] = (va, sa, nva, nsa)
+
+    def quantise(k):
+        G, slot = units[k]
+        va, sa, nva, nsa = acts[k]
+        nm, w = G["name"][slot], width(k)
         V.wait_ge(va, nva)
         V.wait_ge(sa, nsa)
-        if i in pad:
-            V.wait_ge(pad[i], 1)
-        qh = ev()
-        V.quantize_mx(T["hq%d" % i][:, 0:G["nh"]], T["hs%d" % i][:, 0:G["nh"]], h[:, 0:4 * G["nh"]]).then_inc(qh, 1)
-        M.wait_ge(qh, 1)
-        po = T["po%d" % i]
-        done[i] = []
-        for slot in slots:
-            pz = ev()
-            product(pb[i, slot], weights[slot], 512, G, ("hq%d" % i, "hs%d" % i), 0, G["nh"], pz)
-            ce, nce = ev(), 0
-            E = A if i == 0 or slot == 1 else V
-            E.wait_ge(pz, 1)
-            jobs = []
-            if i == 0:
-                m = sum(pc[2] for pc in G["pieces"] if pc[0] != me)
-                if m:
-                    jobs.append((po[:, 0:m], 0, m))
-                if size(me, run(me)):
-                    r0 = rpos[par][run(me)[0]]
-                    jobs.append((T["res%d" % par][:, r0:r0 + G["n"] - m], m, G["n"]))
-            else:
-                jobs = [(po[:, c:c + pc[2]], c, c + pc[2]) for pc, c in zip(G["pieces"], G["hc"]) if pc[3] == slot]
-            for out, a, b in jobs:
-                src = T.z[:, 512 * pb[i, slot] + a:512 * pb[i, slot] + b]
-                if E is A:
-                    A.activation(out, src, ActivationFunctionType.Copy).then_inc(ce, 1)
-                else:
-                    V.tensor_copy(out, src).then_inc(ce, 1)
-                nce += 1
-            done[i].append((ce, nce))
-        if i == 0:
-            done[0] = done[0][0]
+        if (G["i"], slot) in pad:
+            V.wait_ge(pad[G["i"], slot], 1)
+        qhs[k] = ev()
+        V.quantize_mx(T["hq" + nm][:, 0:w], T["hs" + nm][:, 0:w], T["h" + nm][:, 0:4 * w]).then_inc(qhs[k], 1)
 
+    def finish(k):
+        G, slot = units[k]
+        i, nm, po = G["i"], G["name"][slot], T["po%d" % G["i"]]
+        bank = 4 * (k % 2) + 3
+        pz, ce = ev(), ev()
+        M.wait_ge(qhs[k], 1)
+        product(bank, weights[slot], 512, ("hq" + nm, "hs" + nm), 0, width(k), pz)
         if i == 0:
-            g.wait_ge(done[0][0], done[0][1])
-            for pc, c in zip(G["pieces"], G["hc"]):
+            lo, hi = span(G, 0)
+            m, end, jobs = size(me, run(me)), own + tw - lo, []
+            if hi - lo > end:
+                jobs.append((po[:, end:hi - lo], end, hi - lo))
+            if m:
+                r0 = rpos[par][run(me)[0]]
+                jobs.append((T["res%d" % par][:, r0:r0 + m], end - m, end))
+            A.wait_ge(pz, 1)
+            for out, a, b in jobs:
+                A.activation(out, T.z[:, 512 * bank + a:512 * bank + b], ActivationFunctionType.Copy).then_inc(ce, 1)
+        else:
+            V.wait_ge(gbx[i], 1)
+            V.wait_ge(pz, 1)
+            jobs = [(pc[2], c, r) for pc, c, r in zip(G["pieces"], G["hc"], G["rc"]) if pc[3] == slot]
+            for w, c, r in jobs:
+                V.tensor_tensor(po[:, r:r + w], T.z[:, 512 * bank + c:512 * bank + c + w], T["gb%d" % i][:, r:r + w], AluOpType.mult).then_inc(ce, 1)
+        copied[k] = (ce, len(jobs))
+        g.wait_ge(*copied[k])
+        if i == 0:
+            for pc in G["pieces"]:
                 q = pc[0]
                 if q != me:
-                    a = locate(P["ro"][q][par], q, run(me))
-                    copy(q, T["res%d" % par][:, a:a + pc[2]], po[:, c:c + pc[2]], S["pe"])
-        else:
-            for s, c in done[i]:
-                g.wait_ge(s, c)
-            w = max(size(q, farsegs(q, par)) for q in G["ranks"])
-            c, items = 0, []
+                    a, c = locate(P["ro"][q][par], q, run(me)), pc[1] - lo
+                    copy(cores[q], T["res%d" % par][:, a:a + pc[2]], po[:, c:c + pc[2]], S["pe"])
+            if owner[me]:
+                spread(2)
+        elif i == 2:
+            for pc, r in zip(G["pieces"], G["rc"]):
+                if pc[3] == slot:
+                    a = locate(P["ro"][pc[0]][par], pc[0], run(me if slot == 0 else partner))
+                    copy(cores[pc[0]], T["res%d" % par][:, a:a + pc[2]], po[:, r:r + pc[2]], S["pl%d" % par])
+        elif k + 1 == len(units) or units[k + 1][0] is not G:
+            c = 0
             for q in G["ranks"]:
-                a = locate(P["ro"][q][par], q, farsegs(q, par))
-                items.append((q, T["res%d" % par][:, a:a + w], po[:, c:c + w], S["pl%d" % par]))
-                c += size(q, farsegs(q, par))
-            fused(items)
+                a, w = locate(P["ro"][q][par], q, farsegs(q, par)), size(q, farsegs(q, par))
+                copy(cores[q], T["res%d" % par][:, a:a + w], po[:, c:c + w], S["pl%d" % par])
+                c += w
 
-    npe = sum(len(bits(topo.mask(cores[q], core))) for q in grp[me] if q != me and size(me, run(q)))
-    V.wait_ge(gb, 1)
-    V.wait_ge(done[0][0], done[0][1])
+    for k in range(len(units)):
+        first2 = units[k][0]["i"] == 2 and units[k - 1][0] is not units[k][0]
+        ahead = k > 0 and not first2
+        make(k, k - 1 if ahead else None)
+        if ahead:
+            finish(k - 1)
+        if k + 1 == len(units) or units[k + 1][0]["i"] == 2 and units[k + 1][0] is not units[k][0]:
+            quantise(k)
+            finish(k)
+
+    npe = sum(engines(cores[q], core) for q in grp[me] if q != me and size(me, run(q)))
+    if ng:
+        V.wait_ge(gb, 1)
+    V.wait_ge(*copied[0])
     if npe:
         V.wait_ge(S["pe"], npe)
     me_s, nms = ev(), 0
     early = [size(me, P["ro"][me][p][:4]) for p in (0, 1)]
-
-    def gate(p, a, b):
-        r = T["res%d" % p][:, a:b]
-        V.tensor_tensor(r, r, T.gb[:, 128 * p + a:128 * p + b], AluOpType.mult).then_inc(me_s, 1)
-
     for p in (0, 1):
         if early[p]:
-            gate(p, 0, early[p])
+            r = T["res%d" % p][:, 0:early[p]]
+            V.tensor_tensor(r, r, T.gb[:, gpos[p]:gpos[p] + early[p]], AluOpType.mult).then_inc(me_s, 1)
             nms += 1
-    V.wait_ge(me_s, nms)
+    if nms:
+        V.wait_ge(me_s, nms)
     adds = []
     for s in range(n):
         w = cnt[me][s]
@@ -437,12 +498,8 @@ def rank_program(g, core, T, topo):
     add(False)
     for p in (0, 1):
         if early[p] < 128:
-            e = ex[far[me][0]][p]
-            mates = [q for q in grp[me] if owner[q] == owner[me] and size(q, farsegs(q, p))]
-            V.wait_ge(S["pl%d" % p], len(bits(split(topo.mask(cores[e], core), len(mates))[0])))
-            gate(p, early[p], 128)
-            nms += 1
-    V.wait_ge(me_s, nms)
+            calls = 1 if owner[me] else len([e for e in faro if e % 2 == p and size(me, run(e))])
+            V.wait_ge(S["pl%d" % p], calls * engines(cores[ex[faro[0]][p]], core))
     add(True)
     Y.wait_ge(ys, len(adds))
     Y.dma_start(T.y[:, :], T.ysb[:, :]).then_inc(S["st"], 16)

@@ -3,51 +3,41 @@ from concourse.mybir import dt, AluOpType, ActivationFunctionType
 
 F8, U8, BF, F32 = "float8_e4m3fn_x4", "uint8", "bfloat16", "float32"
 C = 0.043
-NV = 80
+NV = 60
 NSIM = 112
 SCRATCH = {
     "xt": ("sbuf", [128, 1024], BF),
     "wt": ("sbuf", [128, 2560], BF),
-    "xq": ("sbuf", [128, 768], F8), "xs": ("sbuf", [128, 768], U8),
+    "xq": ("sbuf", [128, 1024], F8), "xs": ("sbuf", [128, 1024], U8),
     "wq": ("sbuf", [128, 640], F8), "ws": ("sbuf", [128, 640], U8),
-    "pq": ("sbuf", [128, 640], F8), "ps": ("sbuf", [128, 640], U8),
     "rq": ("sbuf", [128, 512], F8), "rs": ("sbuf", [128, 512], U8),
-    "cq1": ("sbuf", [128, 512], F8), "cs1": ("sbuf", [128, 512], U8),
-    "cq2": ("sbuf", [128, 512], F8), "cs2": ("sbuf", [128, 512], U8),
     "gd": ("dram", [128, 2], BF),
     "gr": ("sbuf", [128, 256], BF), "gb": ("sbuf", [128, 256], BF),
     "res0": ("sbuf", [128, 256], F32), "res1": ("sbuf", [128, 256], F32),
-    "po0": ("sbuf", [128, 512], F32),
-    "po1": ("sbuf", [128, 256], F32), "po2": ("sbuf", [128, 256], F32),
+    "po": ("sbuf", [128, 256], F32),
     "ysb": ("sbuf", [128, 128], F32),
     "z": ("psum", [128, 4096], F32),
 }
-for _i in range(4):
+for _i in range(8):
     SCRATCH["ge%d" % _i] = ("dram", [128, 2], BF)
-for _i in (1, 2):
-    SCRATCH["gr%d" % _i] = ("sbuf", [128, 256], BF)
-    SCRATCH["gb%d" % _i] = ("sbuf", [128, 256], BF)
-for _i in ("0", "10", "11", "20", "21"):
-    SCRATCH["h" + _i] = ("sbuf", [128, 2048], BF)
-    SCRATCH["hq" + _i] = ("sbuf", [128, 512], F8)
-    SCRATCH["hs" + _i] = ("sbuf", [128, 512], U8)
-SEMAPHORES = ["lx", "lwa", "lwb", "lwc", "lg", "lgd", "lg1", "lg2", "ga", "gh", "st", "relc", "relp", "xin", "g1", "g2", "wp",
-              "pe", "pl0", "pl1", "ls"] + ["v%d" % i for i in range(NV)]
+for _i in range(2):
+    SCRATCH["h%d" % _i] = ("sbuf", [128, 2048], BF)
+    SCRATCH["hq%d" % _i] = ("sbuf", [128, 512], F8)
+    SCRATCH["hs%d" % _i] = ("sbuf", [128, 512], U8)
+SEMAPHORES = ["lx", "lwa", "lwb", "lwc", "lgd", "lg0", "lg1", "ga", "gh", "tok", "st", "relc", "relp", "xin", "fin", "wa", "wb",
+              "pe", "pl", "ls"] + ["v%d" % i for i in range(NV)]
 
 
 def bits(mask):
     return [i for i in range(32) if mask >> i & 1]
 
 
-def split(mask, k, last=0):
-    b = bits(mask & ~last) + bits(mask & last)
-    n = len(b)
-    sizes = {1: [n], 2: [n // 2] * 2, 3: [n // 2, n // 4, n // 4], 4: [n // 4] * 4}[k]
-    out, a = [], 0
-    for s in sizes:
-        out.append(sum(1 << i for i in b[a:a + s]))
-        a += s
-    return out
+def split(mask, k):
+    b = bits(mask)
+    s = 1
+    while 2 * s * k <= len(b):
+        s *= 2
+    return [sum(1 << i for i in b[s * t:s * t + s]) for t in range(k)]
 
 
 def make_plan(T, topo):
@@ -57,7 +47,6 @@ def make_plan(T, topo):
     grp = [[q for q in range(n) if topo.chip(cores[q]) == topo.chip(cores[r])] for r in range(n)]
     far = [[q for q in range(n) if q not in grp[r]] for r in range(n)]
     owner = [all(topo.may_write(cores[r], cores[q]) for q in far[r]) for r in range(n)]
-    ex = [[[q for q in grp[r] if owner[q] and q % 2 == p][0] for p in (0, 1)] for r in range(n)]
     hp = [[c for c in range(NSIM) if c not in cores and topo.chip(c) == topo.chip(cores[r]) and
            all(topo.may_write(c, cores[q]) for q in far[r])][:2] for r in range(n)]
 
@@ -67,9 +56,6 @@ def make_plan(T, topo):
     def size(j, segs):
         return sum(cnt[j][s] for s in segs)
 
-    def farsegs(j, p):
-        return [s for e in far[j] if e % 2 == p for s in run(e)]
-
     xo = [[(r + k) % n for k in range(n + 1)] for r in range(n)]
 
     def locate(order, j, segs):
@@ -77,73 +63,51 @@ def make_plan(T, topo):
         return size(j, order[:k])
 
     tw = [size(r, xo[r]) for r in range(n)]
-
-    def window(j, dests):
-        dests = [(d, s, l) for d, s, l in dests if size(j, s)]
-        w = max([size(j, s) for d, s, l in dests] + [0])
-        out = []
-        for d, s, l in dests:
-            a, m = locate(xo[j], j, s), size(j, s)
-            st = max(0, a + m - w) if l else min(a, tw[j] - w)
-            out.append((d, st, a - st))
-        return {"w": w, "to": out}
-
-    sends = []
-    for j in range(n):
-        rest = [q for q in grp[j] if q != j]
-        non = [q for q in grp[j] if not owner[q]]
-        if owner[j]:
-            a = window(j, [(cores[ex[far[j][0]][p]], farsegs(j, p), False) for p in (0, 1)])
-        else:
-            a = window(j, [(hp[j][p], farsegs(j, p), j == non[0]) for p in (0, 1)])
-        b = window(j, [(cores[q], run(q), False) for q in [q for q in rest if owner[q]] + [q for q in rest if not owner[q]]])
-        sends.append([a, b])
-
-    def place(c, srcs, k, pos):
-        start, at = {}, {}
-        for q in srcs:
-            for d, st, o in sends[q][k]["to"]:
-                if d == c:
-                    start[q], at[q] = pos, pos + o
-                    pos += sends[q][k]["w"]
-        return start, at, pos
-
-    near = []
-    for r in range(n):
-        own = -tw[r] % 16
-        start, at, end = place(cores[r], [q for q in grp[r] if q != r], 1, own + tw[r])
-        near.append({"own": own, "start": start, "at": at, "end": end})
-    direct, passed, relay = {}, {}, {}
-    for r in range(n):
-        if r != grp[r][0]:
-            continue
-        f = far[r]
-        for p in (0, 1):
-            c, rc = cores[ex[r][p]], hp[f[0]][p]
-            start, at, end = place(c, [q for q in f if owner[q]], 0, 0)
-            direct[c] = {"start": start, "at": at, "w": end}
-            start, at, end = place(rc, [q for q in f if not owner[q]], 0, 0)
-            a = min(at[q] for q in at)
-            b = max(at[q] + size(q, farsegs(q, p)) for q in at)
-            if b - a < 128:
-                b = min(end, a + 128)
-                a = b - 128
-            relay[rc] = {"start": start, "fwd": (a, b), "to": c}
-            passed[c] = {"at": {q: at[q] - a for q in at}, "w": b - a, "relay": rc}
-            for D in (direct[c], passed[c]):
-                D["ranks"] = sorted(D["at"], key=lambda q: size(q, farsegs(q, p)))
+    port, fx = {}, {}
+    for e in range(n):
+        f = far[e]
+        mine = sorted(grp[e], key=lambda q: (owner[q], q))
+        ports = hp[f[0]] + [cores[q] for q in f if owner[q]]
+        port[e] = ports[mine.index(e)]
+        fx[e] = cores[e] if owner[e] else hp[e][mine.index(e)]
+    own, near, fars, rel = [], [], [], []
+    for e in range(n):
+        o = -tw[e] % 16
+        own.append(o)
+        pos, at = o + tw[e], {}
+        for q in grp[e]:
+            if q != e and size(q, run(e)):
+                at[q] = pos
+                pos += size(q, run(e))
+        near.append({"at": at, "end": pos})
+        pos = pos if owner[e] else 0
+        r0, at, rat, wid = pos, {}, {}, {}
+        order = sorted([q for q in far[e] if size(q, run(e))], key=lambda q: cores[q] == port[e])
+        pad = 0 if owner[e] else max(0, 128 - sum(size(q, run(e)) for q in order))
+        if pad:
+            last = [q for q in order if locate(xo[q], q, run(e)) + size(q, run(e)) + pad <= tw[q]][0]
+            order.remove(last)
+            order.append(last)
+        for q in order:
+            at[q] = pos
+            wid[q] = size(q, run(e)) + (pad if q == order[-1] else 0)
+            if cores[q] != port[e]:
+                rat[q] = pos - r0
+            pos += wid[q]
+        fars.append({"at": at, "start": r0, "end": pos - pad, "w": wid})
+        rel.append({"at": rat, "w": sum(wid[q] for q in rat), "to": r0})
     ro = [[[(grp[r][0] - 1 + p + k) % n for k in range(n)] for p in (0, 1)] for r in range(n)]
-    P.update(cores=cores, cnt=cnt, grp=grp, far=far, owner=owner, ex=ex, hp=hp, run=run, size=size, farsegs=farsegs, xo=xo, tw=tw,
-             locate=locate, sends=sends, near=near, direct=direct, passed=passed, relay=relay, ro=ro)
+    P.update(cores=cores, cnt=cnt, grp=grp, far=far, owner=owner, hp=hp, run=run, size=size, xo=xo, tw=tw, port=port, fx=fx,
+             locate=locate, own=own, near=near, fars=fars, rel=rel, ro=ro)
     return P
 
 
 def rank_program(g, core, T, topo):
     P = make_plan(T, topo)
-    n, cores, cnt, grp, far, owner, ex, hp = P["n"], P["cores"], P["cnt"], P["grp"], P["far"], P["owner"], P["ex"], P["hp"]
-    run, size, farsegs, locate, off = P["run"], P["size"], P["farsegs"], P["locate"], P["off"]
+    n, cores, cnt, grp, far, owner, hp, port, fx = [P[k] for k in ("n", "cores", "cnt", "grp", "far", "owner", "hp", "port", "fx")]
+    run, size, locate, off, rel = P["run"], P["size"], P["locate"], P["off"], P["rel"]
     me = T.rank_of(core)
-    if me is None and core not in P["relay"]:
+    if me is None and core not in fx.values():
         return
     S, V, A, M, Y = T.sem, g.vector, g.scalar, g.tensor, g.sync
     count, local = [0], [0]
@@ -155,19 +119,13 @@ def rank_program(g, core, T, topo):
     def engines(s, d):
         return len(bits(topo.mask(s, d)))
 
-    def off_chip(s, d):
-        r = T.rank_of(s)
-        return topo.mask(s, cores[far[r][0]]) if r is not None and owner[r] and topo.chip(s) == topo.chip(d) else 0
-
-    def copy(c, out, in_, sem):
-        a = topo.addr(c)
-        g.remote_dma(out_ap=out, in_ap=in_, remote_sem=sem, local_sem=S["ls"], pid=a[1], routing_id=a[0], dma_engine_mask=topo.mask(core, c))
-        local[0] += engines(core, c)
+    def copy(c, out_, in_, sem, mask=0):
+        a, mask = topo.addr(c), mask or topo.mask(core, c)
+        g.remote_dma(out_ap=out_, in_ap=in_, remote_sem=sem, local_sem=S["ls"], pid=a[1], routing_id=a[0], dma_engine_mask=mask)
+        local[0] += len(bits(mask))
 
     def fused(items):
-        if len(items) == 1:
-            return copy(*items[0])
-        ms = split(topo.mask(core, items[0][0]), len(items), off_chip(core, items[0][0]))
+        ms = split(topo.mask(core, items[0][0]), len(items))
         ts = []
         for (c, o, i, sem), m in zip(items, ms):
             a = topo.addr(c)
@@ -175,332 +133,256 @@ def rank_program(g, core, T, topo):
         g.remote_dma_fused(ts, local_sem=S["ls"])
         local[0] += sum(len(bits(m)) for m in ms)
 
-    def share(c, s, to):
-        ms = split(topo.mask(s, to[0]), len(to), off_chip(s, to[0])) if to else []
-        return sum(len(bits(m)) for d, m in zip(to, ms) if d == c)
+    def share(s, k, d):
+        return len(bits(split(topo.mask(s, d), k)[0]))
 
-    def arrive(c, j, k):
-        return share(c, cores[j], [t[0] for t in P["sends"][j][k]["to"]])
-
-    def gdest(r):
-        return [cores[q] for q in ex[far[r][0]]] if owner[r] else hp[r]
+    def nearmask(s, d):
+        m = topo.mask(cores[s], cores[d])
+        return m & ~topo.mask(cores[s], cores[far[s][0]]) if owner[s] else m
 
     def codes(t, a, b):
         return T[t][:, a:b].bitcast(dt.uint8)
 
+    def gdest(j):
+        return hp[j] + [cores[q] for q in grp[j] if q != j]
+
+    def pass_on():
+        for e in range(n):
+            if port[e] == core and rel[e]["w"]:
+                w, to, k = rel[e]["w"], rel[e]["to"], sum(engines(cores[q], core) for q in rel[e]["at"])
+                g.wait_ge(S["relc"], k)
+                copy(fx[e], codes("xq", to, to + w), codes("rq", 0, w), S["fin"])
+                g.wait_ge(S["relp"], k)
+                copy(fx[e], T.xs[:, to:to + w], T.rs[:, 0:w], S["fin"])
+
+    ex = me if me is not None else [e for e in range(n) if fx[e] == core][0]
+    units = ([0] if me is not None else []) + ([1] if fx[ex] == core else [])
+    par, faro, own, tw = ex % 2, far[ex], P["own"][ex], P["tw"][ex]
+    mine = size(ex, run(ex))
+    a0 = own + tw - mine
+    n1, f0, f1 = P["near"][ex]["end"], P["fars"][ex]["start"], P["fars"][ex]["end"]
+    nearq, farq = P["near"][ex]["at"], P["fars"][ex]["at"]
+    nn = n1 - a0
+    pieces = [[(ex, 0, mine)] + [(q, nearq[q] - a0, size(q, run(ex))) for q in nearq],
+              [(q, nn + farq[q] - f0, size(q, run(ex))) for q in farq]]
+    cols = [(0, nn), (nn, nn + f1 - f0)]
+    spans = [(min(a0, n1 - 128), n1), (min(f0, f1 - 128) if owner[ex] else f0, max(f1, f0 + 128))]
+
+    nx = 0
+    if me is not None:
+        A.dma_start(T.gd[:, :], T.gt[:, :]).then_inc(S["lgd"], 16)
+        two = off[me][n] > off[me][me]
+        for q, a, b, c in [(Y, off[me][me], off[me][n], 0), (A if two else Y, 0, off[me][me + 1], off[me][n] - off[me][me])]:
+            if b > a:
+                q.dma_start(T.xt[:, 4 * c:4 * (c + b - a)], T.x[:, 4 * a:4 * b]).then_inc(S["lx"], 16)
+                nx += 16
+        Y.dma_start(T.wt[:, 0:1024], T.w1[:, 0:1024]).then_inc(S["lwa"], 16)
+        A.dma_start(T.wt[:, 1024:2048], T.w1[:, 1024:2048]).then_inc(S["lwb"], 16)
+        Y.wait_ge(S["tok"], 1)
+        Y.dma_start(T.wt[:, 2048:2560], T.w2[:, :]).then_inc(S["lwc"], 16)
+    ng = {}
+    for u in units:
+        if u == 0:
+            Y.wait_ge(S["ga"], sum(share(cores[q], len(gdest(q)), core) for q in grp[me] if q != me))
+        else:
+            Y.wait_ge(S["gh"], len(faro) * share(hp[faro[0]][0], 2 * len(faro), core))
+        ng[u] = 0
+        for q, c, w in pieces[u]:
+            for k, s in ((1, (ex - 1) % n), (0, ex)):
+                m, a = cnt[q][s], off[q][s]
+                if m and q == me:
+                    Y.dma_start(T.gr[0:1, c:c + m], T.gt[k:k + 1, a:a + m]).then_inc(S["lg%d" % u], 16)
+                elif m:
+                    a = (k * 128 + a) // 2
+                    Y.dma_start(T.gr[0:1, c:c + m], T["ge%d" % q][a:a + m // 2, :]).then_inc(S["lg%d" % u], 16)
+                ng[u] += 16 if m else 0
+                c += m
+
+    qx, qw = ev(), [ev(), ev(), ev()]
+
+    def pack(k):
+        sem, a, b = (("lwa", 0, 256), ("lwb", 256, 512), ("lwc", 512, 640))[k]
+        V.wait_ge(S[sem], 16)
+        V.quantize_mx(T.wq[:, a:b], T.ws[:, a:b], T.wt[:, 4 * a:4 * b]).then_inc(qw[k], 1)
+
+    if me is not None:
+        V.wait_ge(S["lx"], nx)
+        V.quantize_mx(T.xq[:, own:own + tw], T.xs[:, own:own + tw], T.xt[:, 0:4 * tw]).then_inc(qx, 1)
+        pack(0)
+        pack(1)
+        if not owner[me]:
+            pack(2)
+
+    if me is not None:
+        g.wait_ge(S["lgd"], 16)
+        fused([(c, T["ge%d" % me][:, :], T.gd[:, :], S["ga"]) for c in gdest(me)])
+        g.wait_ge(qx, 1)
+
+        def src(plane, e, w):
+            a = own + locate(P["xo"][me], me, run(e))
+            return T.xs[:, a:a + w] if plane else codes("xq", a, a + w)
+
+        def dst(plane, bufs, a, w):
+            return T[bufs[1]][:, a:a + w] if plane else codes(bufs[0], a, a + w)
+
+        def send_near(to):
+            for e in grp[me]:
+                w = size(me, run(e))
+                if e != me and w and owner[e] == to:
+                    for plane in (0, 1):
+                        copy(cores[e], dst(plane, ("xq", "xs"), P["near"][e]["at"][me], w), src(plane, e, w), S["xin"], nearmask(me, e))
+
+        def send_weights(a, b, ks, sem):
+            for k in ks:
+                g.wait_ge(qw[k], 1)
+            copy(fx[me], codes("wq", a, b), codes("wq", a, b), sem)
+            copy(fx[me], T.ws[:, a:b], T.ws[:, a:b], sem)
+
+        fo = sorted([e for e in faro if size(me, run(e))], key=lambda e: (owner[e], e))
+        for plane in (0, 1):
+            for e in fo:
+                w = P["fars"][e]["w"][me]
+                if port[e] == core:
+                    copy(fx[e], dst(plane, ("xq", "xs"), P["fars"][e]["at"][me], w), src(plane, e, w), S["fin"])
+                else:
+                    copy(port[e], dst(plane, ("rq", "rs"), rel[e]["at"][me], w), src(plane, e, w), S["relp" if plane else "relc"])
+        if owner[me]:
+            g.sem_inc(S["tok"], 1)
+            send_near(True)
+            send_near(False)
+            pass_on()
+        else:
+            send_near(True)
+            send_weights(0, 512, (0, 1), S["wa"])
+            g.sem_inc(S["tok"], 1)
+            send_near(False)
+            send_weights(512, 640, (2,), S["wb"])
+    else:
+        home, there = grp[ex], far[ex]
+        g.wait_ge(S["ga"], sum(share(cores[q], len(gdest(q)), core) for q in home))
+        to = [e for k, e in enumerate(there) if k % 2 == hp[ex].index(core)]
+        fused([(fx[e], T["ge%d" % q][:, :], T["ge%d" % q][:, :], S["gh"]) for e in to for q in home])
+        pass_on()
+    gb = [ev(), ev()]
+    for u in units:
+        a, b = cols[u]
+        if b > a:
+            g.wait_ge(S["lg%d" % u], ng[u])
+            g.partition_broadcast(T.gb[:, a:b], T.gr[0:1, a:b], 128).then_inc(gb[u], 1)
+
+    nxin = sum(2 * len(bits(nearmask(q, ex))) for q in nearq)
+    nfin = sum(2 * engines(cores[q], core) for q in farq if cores[q] == port[ex]) + (2 * engines(port[ex], core) if rel[ex]["w"] else 0)
+    if me is not None:
+        arrived = [(qw[0], 1), (qw[1], 1), (qw[2], 1)]
+    else:
+        k = 2 * engines(cores[ex], core)
+        arrived = [(S["wa"], k), (S["wa"], k), (S["wb"], k)]
+    qhs, acts, done, zs, pz, weights = {}, {}, {}, {}, [ev(), ev()], [0]
+
+    def product(bank, k, buf, lo, hi, sem):
+        while weights[0] < min(k // 2 + 1, 3):
+            M.wait_ge(*arrived[weights[0]])
+            weights[0] += 1
+        M.matmul_mx(T.z[:, 512 * bank:512 * bank + hi - lo], T.wq[:, 128 * k:128 * k + 128], T.ws[:, 128 * k:128 * k + 128],
+                    T[buf[0]][:, lo:hi], T[buf[1]][:, lo:hi], True, True).then_inc(sem, 1)
+
+    def make(i):
+        lo, hi = spans[i]
+        w, va, sa = hi - lo, ev(), ev()
+        if i == 0:
+            M.wait_ge(qx, 1)
+            if nxin:
+                M.wait_ge(S["xin"], nxin)
+        elif nfin:
+            M.wait_ge(S["fin"], nfin)
+        for b in range(4):
+            bank = 4 * i + b
+            zs[i, b] = ev()
+            product(bank, b, ("xq", "xs"), lo, hi, zs[i, b])
+            E, z, o = (V, A)[b % 2], T.z[:, 512 * bank:512 * bank + w], T["h%d" % i][:, b:4 * w:4]
+            E.wait_ge(zs[i, b], 1)
+            if b % 2 == 0:
+                V.tensor_scalar(o, z, 0.0, C, AluOpType.max, AluOpType.mult).then_inc(va, 1)
+            else:
+                A.activation(o, z, ActivationFunctionType.Relu, scale=C).then_inc(sa, 1)
+        acts[i] = (va, sa)
+
+    def quantise(i):
+        w = spans[i][1] - spans[i][0]
+        V.wait_ge(acts[i][0], 2)
+        V.wait_ge(acts[i][1], 2)
+        qhs[i] = ev()
+        V.quantize_mx(T["hq%d" % i][:, 0:w], T["hs%d" % i][:, 0:w], T["h%d" % i][:, 0:4 * w]).then_inc(qhs[i], 1)
+
+    def last(i):
+        M.wait_ge(qhs[i], 1)
+        product(4 * i, 4, ("hq%d" % i, "hs%d" % i), 0, spans[i][1] - spans[i][0], pz[i])
+
+    def gated(i):
+        a, b = cols[i]
+        z0 = 512 * 4 * i + (f0 - nn if i else a0) - spans[i][0]
+        ce, jobs = ev(), []
+        if i == 0 and mine:
+            r0 = locate(P["ro"][me][par], me, run(me))
+            jobs.append((T["res%d" % par][:, r0:r0 + mine], 0, mine))
+            a = mine
+        if b > a:
+            jobs.append((T.po[:, a:b], a, b))
+        if jobs:
+            V.wait_ge(gb[i], 1)
+        V.wait_ge(pz[i], 1)
+        for o, a, b in jobs:
+            V.tensor_tensor(o, T.z[:, z0 + a:z0 + b], T.gb[:, a:b], AluOpType.mult).then_inc(ce, 1)
+        done[i] = (ce, len(jobs))
+
+    def leave(i):
+        g.wait_ge(*done[i])
+        for q, c, w in sorted(pieces[i], key=lambda t: -t[2]):
+            if q != ex:
+                a = locate(P["ro"][q][par], q, run(ex))
+                copy(cores[q], T["res%d" % par][:, a:a + w], T.po[:, c:c + w], S["pl" if i else "pe"])
+
+    if len(units) == 1:
+        for step in (make, quantise, last, gated, leave):
+            step(units[0])
+    else:
+        make(0)
+        pack(2)
+        make(1)
+        for u in units:
+            quantise(u)
+            last(u)
+        gated(0)
+        gated(1)
+        leave(0)
+        leave(1)
     if me is None:
-        R = P["relay"][core]
-        a, b = R["fwd"]
-        home = [r for r in range(n) if topo.chip(cores[r]) == topo.chip(core)]
-        src = [q for q in home if not owner[q]]
-        g.wait_ge(S["ga"], sum(share(core, cores[q], gdest(q)) for q in src))
-        fused([(R["to"], T["ge%d" % home.index(q)][:, :], T["ge%d" % home.index(q)][:, :], S["gh"]) for q in src])
-        nrel = sum(arrive(core, q, 0) for q in R["start"])
-        g.wait_ge(S["relc"], nrel)
-        copy(R["to"], codes("cq2", 0, b - a), codes("rq", a, b), S["g2"])
-        g.wait_ge(S["relp"], nrel)
-        copy(R["to"], T.cs2[:, 0:b - a], T.rs[:, a:b], S["g2"])
         g.wait_ge(S["ls"], local[0])
         return
 
-    par, faro = me % 2, far[me]
-    weights = [("wq", "ws"), ("pq", "ps")]
-
-    lay = P["near"][me]
-    own, tw = lay["own"], P["tw"][me]
-    pieces = []
-    for q in [q for q in grp[me] if q != me] + [me]:
-        w = size(q, run(me))
-        if w:
-            pieces.append((q, own + locate(P["xo"][me], me, run(me)) if q == me else lay["at"][q], w, 0))
-    groups = [{"q": "xq", "s": "xs", "w": lay["end"], "pieces": pieces, "i": 0}]
-    duo = [e for e in grp[me] if e % 2 == par]
-    partner = [e for e in duo if e != me][0]
-    for i, D in enumerate([P["direct"][core], P["passed"][core]] if owner[me] else []):
-        pieces = []
-        for q in D["ranks"]:
-            c = D["at"][q]
-            for e in duo:
-                w = size(q, run(e))
-                if w:
-                    pieces.append((q, c, w, 0 if e == me else 1))
-                c += w
-        groups.append({"q": "cq%d" % (i + 1), "s": "cs%d" % (i + 1), "w": D["w"], "pieces": pieces, "ranks": D["ranks"], "i": i + 1})
-    for G in groups:
-        c, ht, hc, rc = 0, {}, [], []
-        for pc in G["pieces"]:
-            hc.append(ht.get(pc[3], 0))
-            ht[pc[3]] = hc[-1] + pc[2]
-            rc.append(c)
-            c += pc[2]
-        G["hc"], G["rc"], G["n"], G["ht"] = hc, rc, c, ht
-        G["name"] = {sl: "0" if G["i"] == 0 else "%d%d" % (G["i"], sl) for sl in ht}
-
-    def span(G, slot):
-        cs = [(pc[1], pc[1] + pc[2]) for pc in G["pieces"] if pc[3] == slot]
-        lo, hi = min(a for a, b in cs), max(b for a, b in cs)
-        if hi - lo < 128:
-            lo = max(0, min(lo, G["w"] - 128))
-            hi = max(hi, lo + 128)
-        return lo, hi
-
-    pad = {}
-    for G in groups[1:]:
-        for sl in sorted(G["ht"]):
-            if G["ht"][sl] < 128:
-                pad[G["i"], sl] = ev()
-                V.memset(T["h" + G["name"][sl]][:, 4 * G["ht"][sl]:512], 0.0).then_inc(pad[G["i"], sl], 1)
-
-    A.dma_start(T.gd[:, :], T.gt[:, :]).then_inc(S["lgd"], 16)
-    nx = 0
-    for q, a, b, c in [(Y, off[me][me], off[me][n], 0), (A, 0, off[me][me + 1], off[me][n] - off[me][me])]:
-        if b > a:
-            q.dma_start(T.xt[:, 4 * c:4 * (c + b - a)], T.x[:, 4 * a:4 * b]).then_inc(S["lx"], 16)
-            nx += 16
-    rpos, gates, gpos = [], [], [0]
-    for p in (0, 1):
-        pos, c = {}, 0
-        for k, s in enumerate(P["ro"][me][p]):
-            pos[s] = c
-            w = cnt[me][s]
-            if w and k < 4:
-                gates.append((gpos[p] + c, 0 if s % 2 == p else 1, off[me][s], w))
-            c += w
-        rpos.append(pos)
-        gpos.append(gpos[p] + size(me, P["ro"][me][p][:4]))
-    ng = 16 * len(gates)
-
-    def gate_loads(q, some):
-        for c, i, a, w in some:
-            q.dma_start(T.gr[0:1, c:c + w], T.gt[i:i + 1, a:a + w]).then_inc(S["lg"], 16)
-
-    few = 0 if off[me][me + 1] else 3
-    gate_loads(A, gates[:few])
-    Y.dma_start(T.wt[:, 0:1024], T.w1[:, 0:1024]).then_inc(S["lwa"], 16)
-    A.dma_start(T.wt[:, 1024:2048], T.w1[:, 1024:2048]).then_inc(S["lwb"], 16)
-    Y.dma_start(T.wt[:, 2048:2560], T.w2[:, :]).then_inc(S["lwc"], 16)
-    gate_loads(Y, gates[few:])
-
-    V.wait_ge(S["lx"], nx)
-    qx, qw = ev(), ev()
-    V.quantize_mx(T.xq[:, own:own + tw], T.xs[:, own:own + tw], T.xt[:, 0:4 * tw]).then_inc(qx, 1)
-    for sem, a, b in (("lwa", 0, 256), ("lwb", 256, 512), ("lwc", 512, 640)):
-        V.wait_ge(S[sem], 16)
-        V.quantize_mx(T.wq[:, a:b], T.ws[:, a:b], T.wt[:, 4 * a:4 * b]).then_inc(qw, 1)
-
-    g.wait_ge(S["lgd"], 16)
-    slot_g = "ge%d" % grp[me].index(me)
-    fused([(c, T[slot_g][:, :], T.gd[:, :], S["ga"]) for c in gdest(me)])
-    g.wait_ge(qx, 1)
-    for k, send in enumerate(P["sends"][me]):
-        w = send["w"]
-        for plane in (0, 1):
-            items = []
-            for c, st, o in send["to"]:
-                if k == 1:
-                    at, buf, sem = P["near"][cores.index(c)]["start"][me], ("xs", "xq"), "xin"
-                elif owner[me]:
-                    at, buf, sem = P["direct"][c]["start"][me], ("cs1", "cq1"), "g1"
-                else:
-                    at, buf, sem = P["relay"][c]["start"][me], ("rs", "rq"), ("relp" if plane else "relc")
-                if plane:
-                    items.append((c, T[buf[0]][:, at:at + w], T.xs[:, own + st:own + st + w], S[sem]))
-                else:
-                    items.append((c, codes(buf[1], at, at + w), codes("xq", own + st, own + st + w), S[sem]))
-            if items:
-                fused(items)
-    if not owner[me]:
-        g.wait_ge(qw, 3)
-        c = cores[ex[me][par]]
-        copy(c, codes("pq", 0, 640), codes("wq", 0, 640), S["wp"])
-        copy(c, T.ps[:, 0:640], T.ws[:, 0:640], S["wp"])
-    gb = ev()
-    if ng:
-        g.wait_ge(S["lg"], ng)
-        g.partition_broadcast(T.gb[:, 0:gpos[2]], T.gr[0:1, 0:gpos[2]], 128).then_inc(gb, 1)
-    gbx, ngx = {}, {}
-    for G in groups[1:]:
-        i, nl = G["i"], 0
-        if i == 1:
-            Y.wait_ge(S["ga"], sum(share(core, cores[q], gdest(q)) for q in faro if owner[q]))
-        else:
-            Y.wait_ge(S["gh"], engines(P["passed"][core]["relay"], core))
-        for (q, c, w, sl), r in zip(G["pieces"], G["rc"]):
-            e = me if sl == 0 else partner
-            for k, s in ((1, (e - 1) % n), (0, e)):
-                m, src = cnt[q][s], T["ge%d" % faro.index(q)]
-                if m:
-                    a = (k * 128 + off[q][s]) // 2
-                    Y.dma_start(T["gr%d" % i][0:1, r:r + m], src[a:a + m // 2, :]).then_inc(S["lg%d" % i], 16)
-                    nl += 16
-                r += m
-        gbx[i], ngx[i] = ev(), nl
-
-    def spread(i):
-        g.wait_ge(S["lg%d" % i], ngx[i])
-        g.partition_broadcast(T["gb%d" % i][:, 0:groups[i]["n"]], T["gr%d" % i][0:1, 0:groups[i]["n"]], 128).then_inc(gbx[i], 1)
-
-    if owner[me]:
-        spread(1)
-
-    M.wait_ge(qw, 3)
-    M.wait_ge(qx, 1)
-    nxin = sum(2 * arrive(core, q, 1) for q in grp[me] if q != me)
-    if nxin:
-        M.wait_ge(S["xin"], nxin)
-    units = [(G, sl) for G in groups for sl in sorted(G["ht"], key=lambda sl: -G["ht"][sl] if G["i"] == 2 else sl)]
-    acts, qhs, copied = {}, {}, {}
-
-    def product(bank, wt, a, buf, lo, hi, sem):
-        M.matmul_mx(T.z[:, 512 * bank:512 * bank + hi - lo], T[wt[0]][:, a:a + 128], T[wt[1]][:, a:a + 128],
-                    T[buf[0]][:, lo:hi], T[buf[1]][:, lo:hi], True, True).then_inc(sem, 1)
-
-    def width(k):
-        G, slot = units[k]
-        return max(128, G["ht"][slot]) if G["i"] else span(G, 0)[1] - span(G, 0)[0]
-
-    def make(k, between):
-        G, slot = units[k]
-        i, h = G["i"], T["h" + G["name"][slot]]
-        lo, hi = span(G, slot)
-        if i == 1 and units[k - 1][0] is not G:
-            M.wait_ge(S["g1"], sum(2 * arrive(core, q, 0) for q in faro if owner[q]))
-        if i == 2 and units[k - 1][0] is not G:
-            M.wait_ge(S["g2"], 2 * engines(P["passed"][core]["relay"], core))
-        if i == 1 and slot == 1:
-            M.wait_ge(S["wp"], 2 * engines(cores[partner], core))
-        if i:
-            todo = [(pc[1] - lo, pc[2], c) for pc, c in zip(G["pieces"], G["hc"]) if pc[3] == slot]
-        else:
-            todo = [(0, hi - lo, 0)]
-        va, sa, nva, nsa = ev(), ev(), 0, 0
-        for b in (0, 2, 1, 3):
-            bank = 4 * (k % 2) + b
-            if b == 3 and k > 1:
-                M.wait_ge(*copied[k - 2])
-            zs = ev()
-            product(bank, weights[slot], 128 * b, (G["q"], G["s"]), lo, hi, zs)
-            E = V if b < 2 else A
-            E.wait_ge(zs, 1)
-            for a, w, c in todo:
-                src = T.z[:, 512 * bank + a:512 * bank + a + w]
-                out = h[:, 4 * c + b:4 * (c + w):4]
-                if b < 2:
-                    V.tensor_scalar(out, src, 0.0, C, AluOpType.max, AluOpType.mult).then_inc(va, 1)
-                    nva += 1
-                else:
-                    A.activation(out, src, ActivationFunctionType.Relu, scale=C).then_inc(sa, 1)
-                    nsa += 1
-            if b == 0 and between is not None:
-                quantise(between)
-        acts[k] = (va, sa, nva, nsa)
-
-    def quantise(k):
-        G, slot = units[k]
-        va, sa, nva, nsa = acts[k]
-        nm, w = G["name"][slot], width(k)
-        V.wait_ge(va, nva)
-        V.wait_ge(sa, nsa)
-        if (G["i"], slot) in pad:
-            V.wait_ge(pad[G["i"], slot], 1)
-        qhs[k] = ev()
-        V.quantize_mx(T["hq" + nm][:, 0:w], T["hs" + nm][:, 0:w], T["h" + nm][:, 0:4 * w]).then_inc(qhs[k], 1)
-
-    def finish(k):
-        G, slot = units[k]
-        i, nm, po = G["i"], G["name"][slot], T["po%d" % G["i"]]
-        bank = 4 * (k % 2) + 3
-        pz, ce = ev(), ev()
-        M.wait_ge(qhs[k], 1)
-        product(bank, weights[slot], 512, ("hq" + nm, "hs" + nm), 0, width(k), pz)
-        if i == 0:
-            lo, hi = span(G, 0)
-            m, end, jobs = size(me, run(me)), own + tw - lo, []
-            if hi - lo > end:
-                jobs.append((po[:, end:hi - lo], end, hi - lo))
-            if m:
-                r0 = rpos[par][run(me)[0]]
-                jobs.append((T["res%d" % par][:, r0:r0 + m], end - m, end))
-            A.wait_ge(pz, 1)
-            for out, a, b in jobs:
-                A.activation(out, T.z[:, 512 * bank + a:512 * bank + b], ActivationFunctionType.Copy).then_inc(ce, 1)
-        else:
-            V.wait_ge(gbx[i], 1)
-            V.wait_ge(pz, 1)
-            jobs = [(pc[2], c, r) for pc, c, r in zip(G["pieces"], G["hc"], G["rc"]) if pc[3] == slot]
-            for w, c, r in jobs:
-                V.tensor_tensor(po[:, r:r + w], T.z[:, 512 * bank + c:512 * bank + c + w], T["gb%d" % i][:, r:r + w], AluOpType.mult).then_inc(ce, 1)
-        copied[k] = (ce, len(jobs))
-        g.wait_ge(*copied[k])
-        if i == 0:
-            for pc in G["pieces"]:
-                q = pc[0]
-                if q != me:
-                    a, c = locate(P["ro"][q][par], q, run(me)), pc[1] - lo
-                    copy(cores[q], T["res%d" % par][:, a:a + pc[2]], po[:, c:c + pc[2]], S["pe"])
-            if owner[me]:
-                spread(2)
-        elif i == 2:
-            for pc, r in zip(G["pieces"], G["rc"]):
-                if pc[3] == slot:
-                    a = locate(P["ro"][pc[0]][par], pc[0], run(me if slot == 0 else partner))
-                    copy(cores[pc[0]], T["res%d" % par][:, a:a + pc[2]], po[:, r:r + pc[2]], S["pl%d" % par])
-        elif k + 1 == len(units) or units[k + 1][0] is not G:
-            c = 0
-            for q in G["ranks"]:
-                a, w = locate(P["ro"][q][par], q, farsegs(q, par)), size(q, farsegs(q, par))
-                copy(cores[q], T["res%d" % par][:, a:a + w], po[:, c:c + w], S["pl%d" % par])
-                c += w
-
-    for k in range(len(units)):
-        first2 = units[k][0]["i"] == 2 and units[k - 1][0] is not units[k][0]
-        ahead = k > 0 and not first2
-        make(k, k - 1 if ahead else None)
-        if ahead:
-            finish(k - 1)
-        if k + 1 == len(units) or units[k + 1][0]["i"] == 2 and units[k + 1][0] is not units[k][0]:
-            quantise(k)
-            finish(k)
-
     npe = sum(engines(cores[q], core) for q in grp[me] if q != me and size(me, run(q)))
-    if ng:
-        V.wait_ge(gb, 1)
-    V.wait_ge(*copied[0])
-    if npe:
-        V.wait_ge(S["pe"], npe)
-    me_s, nms = ev(), 0
-    early = [size(me, P["ro"][me][p][:4]) for p in (0, 1)]
-    for p in (0, 1):
-        if early[p]:
-            r = T["res%d" % p][:, 0:early[p]]
-            V.tensor_tensor(r, r, T.gb[:, gpos[p]:gpos[p] + early[p]], AluOpType.mult).then_inc(me_s, 1)
-            nms += 1
-    if nms:
-        V.wait_ge(me_s, nms)
+    npl = sum(engines(fx[q], core) for q in faro if size(me, run(q)))
     adds = []
     for s in range(n):
         w = cnt[me][s]
         if not w:
             continue
-        late = any(P["ro"][me][p].index(s) >= 4 for p in (0, 1))
-        a0, a1, y0 = rpos[0][s], rpos[1][s], off[me][s]
-        if adds and adds[-1][0] == late and adds[-1][1] + adds[-1][4] == a0 and adds[-1][2] + adds[-1][4] == a1:
+        late = s in faro or (s + 1) % n in faro
+        b0, b1 = [locate(P["ro"][me][p], me, [s]) for p in (0, 1)]
+        if adds and adds[-1][0] == late and adds[-1][1] + adds[-1][4] == b0 and adds[-1][2] + adds[-1][4] == b1:
             adds[-1][4] += w
         else:
-            adds.append([late, a0, a1, y0, w])
+            adds.append([late, b0, b1, off[me][s], w])
     ys = ev()
-
-    def add(late):
-        for l, a0, a1, y0, w in adds:
+    V.wait_ge(*done[0])
+    if npe:
+        V.wait_ge(S["pe"], npe)
+    for late in (False, True):
+        if late and npl:
+            V.wait_ge(S["pl"], npl)
+        for l, b0, b1, y0, w in adds:
             if l == late:
-                V.tensor_tensor(T.ysb[:, y0:y0 + w], T.res0[:, a0:a0 + w], T.res1[:, a1:a1 + w], AluOpType.add).then_inc(ys, 1)
-
-    add(False)
-    for p in (0, 1):
-        if early[p] < 128:
-            calls = 1 if owner[me] else len([e for e in faro if e % 2 == p and size(me, run(e))])
-            V.wait_ge(S["pl%d" % p], calls * engines(cores[ex[faro[0]][p]], core))
-    add(True)
+                V.tensor_tensor(T.ysb[:, y0:y0 + w], T.res0[:, b0:b0 + w], T.res1[:, b1:b1 + w], AluOpType.add).then_inc(ys, 1)
     Y.wait_ge(ys, len(adds))
     Y.dma_start(T.y[:, :], T.ysb[:, :]).then_inc(S["st"], 16)
     Y.wait_ge(S["st"], 16)

from concourse.bass import DstId, RemoteDMATransfer
from concourse.mybir import dt, AluOpType, ActivationFunctionType

F8, U8, BF, F32 = "float8_e4m3fn_x4", "uint8", "bfloat16", "float32"
C = 0.043
NV = 60
NSIM = 112
SCRATCH = {
    "xt": ("sbuf", [128, 1024], BF),
    "wt": ("sbuf", [128, 2560], BF),
    "xq": ("sbuf", [128, 1024], F8), "xs": ("sbuf", [128, 1024], U8),
    "wq": ("sbuf", [128, 640], F8), "ws": ("sbuf", [128, 640], U8),
    "rq": ("sbuf", [128, 512], F8), "rs": ("sbuf", [128, 512], U8),
    "gd": ("dram", [128, 2], BF),
    "gr": ("sbuf", [128, 256], BF), "gb": ("sbuf", [128, 256], BF),
    "res0": ("sbuf", [128, 256], F32), "res1": ("sbuf", [128, 256], F32),
    "po": ("sbuf", [128, 256], F32),
    "ysb": ("sbuf", [128, 128], F32),
    "z": ("psum", [128, 4096], F32),
}
for _i in range(8):
    SCRATCH["ge%d" % _i] = ("dram", [128, 2], BF)
for _i in range(2):
    SCRATCH["h%d" % _i] = ("sbuf", [128, 2048], BF)
    SCRATCH["hq%d" % _i] = ("sbuf", [128, 512], F8)
    SCRATCH["hs%d" % _i] = ("sbuf", [128, 512], U8)
SEMAPHORES = ["lx", "lwa", "lwb", "lwc", "lgd", "lg0", "lg1", "ga", "gh", "tok", "st", "relc", "relp", "xin", "fin", "wa", "wb",
              "pe", "pl", "ls"] + ["v%d" % i for i in range(NV)]


def bits(mask):
    return [i for i in range(32) if mask >> i & 1]


def split(mask, k):
    b = bits(mask)
    s = 1
    while 2 * s * k <= len(b):
        s *= 2
    return [sum(1 << i for i in b[s * t:s * t + s]) for t in range(k)]


def make_plan(T, topo):
    cores, cnt = T.cores, T.tables["CNT"]
    n = len(cores)
    P = {"n": n, "off": [[sum(c[:e]) for e in range(n + 1)] for c in cnt]}
    grp = [[q for q in range(n) if topo.chip(cores[q]) == topo.chip(cores[r])] for r in range(n)]
    far = [[q for q in range(n) if q not in grp[r]] for r in range(n)]
    owner = [all(topo.may_write(cores[r], cores[q]) for q in far[r]) for r in range(n)]
    hp = [[c for c in range(NSIM) if c not in cores and topo.chip(c) == topo.chip(cores[r]) and
           all(topo.may_write(c, cores[q]) for q in far[r])][:2] for r in range(n)]

    def run(e):
        return [(e - 1) % n, e]

    def size(j, segs):
        return sum(cnt[j][s] for s in segs)

    xo = [[(r + k) % n for k in range(n + 1)] for r in range(n)]

    def locate(order, j, segs):
        k = [i for i in range(len(order)) if order[i:i + len(segs)] == segs][0]
        return size(j, order[:k])

    tw = [size(r, xo[r]) for r in range(n)]
    port, fx = {}, {}
    for e in range(n):
        f = far[e]
        mine = sorted(grp[e], key=lambda q: (owner[q], q))
        ports = hp[f[0]] + [cores[q] for q in f if owner[q]]
        port[e] = ports[mine.index(e)]
        fx[e] = cores[e] if owner[e] else hp[e][mine.index(e)]
    own, near, fars, rel = [], [], [], []
    for e in range(n):
        o = -tw[e] % 16
        own.append(o)
        pos, at = o + tw[e], {}
        for q in grp[e]:
            if q != e and size(q, run(e)):
                at[q] = pos
                pos += size(q, run(e))
        near.append({"at": at, "end": pos})
        pos = pos if owner[e] else 0
        r0, at, rat, wid = pos, {}, {}, {}
        order = sorted([q for q in far[e] if size(q, run(e))], key=lambda q: cores[q] == port[e])
        pad = 0 if owner[e] else max(0, 128 - sum(size(q, run(e)) for q in order))
        if pad:
            last = [q for q in order if locate(xo[q], q, run(e)) + size(q, run(e)) + pad <= tw[q]][0]
            order.remove(last)
            order.append(last)
        for q in order:
            at[q] = pos
            wid[q] = size(q, run(e)) + (pad if q == order[-1] else 0)
            if cores[q] != port[e]:
                rat[q] = pos - r0
            pos += wid[q]
        fars.append({"at": at, "start": r0, "end": pos - pad, "w": wid})
        rel.append({"at": rat, "w": sum(wid[q] for q in rat), "to": r0})
    ro = [[[(grp[r][0] - 1 + p + k) % n for k in range(n)] for p in (0, 1)] for r in range(n)]
    P.update(cores=cores, cnt=cnt, grp=grp, far=far, owner=owner, hp=hp, run=run, size=size, xo=xo, tw=tw, port=port, fx=fx,
             locate=locate, own=own, near=near, fars=fars, rel=rel, ro=ro)
    return P


def rank_program(g, core, T, topo):
    P = make_plan(T, topo)
    n, cores, cnt, grp, far, owner, hp, port, fx = [P[k] for k in ("n", "cores", "cnt", "grp", "far", "owner", "hp", "port", "fx")]
    run, size, locate, off, rel = P["run"], P["size"], P["locate"], P["off"], P["rel"]
    me = T.rank_of(core)
    if me is None and core not in fx.values():
        return
    S, V, A, M, Y = T.sem, g.vector, g.scalar, g.tensor, g.sync
    count, local = [0], [0]

    def ev():
        count[0] += 1
        return S["v%d" % (count[0] - 1)]

    def engines(s, d):
        return len(bits(topo.mask(s, d)))

    def copy(c, out_, in_, sem, mask=0):
        a, mask = topo.addr(c), mask or topo.mask(core, c)
        g.remote_dma(out_ap=out_, in_ap=in_, remote_sem=sem, local_sem=S["ls"], pid=a[1], routing_id=a[0], dma_engine_mask=mask)
        local[0] += len(bits(mask))

    def fused(items):
        ms = split(topo.mask(core, items[0][0]), len(items))
        ts = []
        for (c, o, i, sem), m in zip(items, ms):
            a = topo.addr(c)
            ts.append(RemoteDMATransfer(dst_ids=[DstId(rid=a[0], pnc=a[1])], dma_engine_mask=m, remote_sem=sem, src=i, dst=o))
        g.remote_dma_fused(ts, local_sem=S["ls"])
        local[0] += sum(len(bits(m)) for m in ms)

    def share(s, k, d):
        return len(bits(split(topo.mask(s, d), k)[0]))

    def nearmask(s, d):
        m = topo.mask(cores[s], cores[d])
        return m & ~topo.mask(cores[s], cores[far[s][0]]) if owner[s] else m

    def codes(t, a, b):
        return T[t][:, a:b].bitcast(dt.uint8)

    def gdest(j):
        return hp[j] + [cores[q] for q in grp[j] if q != j]

    def pass_on():
        for e in range(n):
            if port[e] == core and rel[e]["w"]:
                w, to, k = rel[e]["w"], rel[e]["to"], sum(engines(cores[q], core) for q in rel[e]["at"])
                g.wait_ge(S["relc"], k)
                copy(fx[e], codes("xq", to, to + w), codes("rq", 0, w), S["fin"])
                g.wait_ge(S["relp"], k)
                copy(fx[e], T.xs[:, to:to + w], T.rs[:, 0:w], S["fin"])

    ex = me if me is not None else [e for e in range(n) if fx[e] == core][0]
    units = ([0] if me is not None else []) + ([1] if fx[ex] == core else [])
    par, faro, own, tw = ex % 2, far[ex], P["own"][ex], P["tw"][ex]
    mine = size(ex, run(ex))
    a0 = own + tw - mine
    n1, f0, f1 = P["near"][ex]["end"], P["fars"][ex]["start"], P["fars"][ex]["end"]
    nearq, farq = P["near"][ex]["at"], P["fars"][ex]["at"]
    nn = n1 - a0
    pieces = [[(ex, 0, mine)] + [(q, nearq[q] - a0, size(q, run(ex))) for q in nearq],
              [(q, nn + farq[q] - f0, size(q, run(ex))) for q in farq]]
    cols = [(0, nn), (nn, nn + f1 - f0)]
    spans = [(min(a0, n1 - 128), n1), (min(f0, f1 - 128) if owner[ex] else f0, max(f1, f0 + 128))]

    nx = 0
    if me is not None:
        A.dma_start(T.gd[:, :], T.gt[:, :]).then_inc(S["lgd"], 16)
        two = off[me][n] > off[me][me]
        for q, a, b, c in [(Y, off[me][me], off[me][n], 0), (A if two else Y, 0, off[me][me + 1], off[me][n] - off[me][me])]:
            if b > a:
                q.dma_start(T.xt[:, 4 * c:4 * (c + b - a)], T.x[:, 4 * a:4 * b]).then_inc(S["lx"], 16)
                nx += 16
        Y.dma_start(T.wt[:, 0:1024], T.w1[:, 0:1024]).then_inc(S["lwa"], 16)
        A.dma_start(T.wt[:, 1024:2048], T.w1[:, 1024:2048]).then_inc(S["lwb"], 16)
        Y.wait_ge(S["tok"], 1)
        Y.dma_start(T.wt[:, 2048:2560], T.w2[:, :]).then_inc(S["lwc"], 16)
    ng = {}
    for u in units:
        if u == 0:
            Y.wait_ge(S["ga"], sum(share(cores[q], len(gdest(q)), core) for q in grp[me] if q != me))
        else:
            Y.wait_ge(S["gh"], len(faro) * share(hp[faro[0]][0], 2 * len(faro), core))
        ng[u] = 0
        for q, c, w in pieces[u]:
            for k, s in ((1, (ex - 1) % n), (0, ex)):
                m, a = cnt[q][s], off[q][s]
                if m and q == me:
                    Y.dma_start(T.gr[0:1, c:c + m], T.gt[k:k + 1, a:a + m]).then_inc(S["lg%d" % u], 16)
                elif m:
                    a = (k * 128 + a) // 2
                    Y.dma_start(T.gr[0:1, c:c + m], T["ge%d" % q][a:a + m // 2, :]).then_inc(S["lg%d" % u], 16)
                ng[u] += 16 if m else 0
                c += m

    qx, qw = ev(), [ev(), ev(), ev()]

    def pack(k):
        sem, a, b = (("lwa", 0, 256), ("lwb", 256, 512), ("lwc", 512, 640))[k]
        V.wait_ge(S[sem], 16)
        V.quantize_mx(T.wq[:, a:b], T.ws[:, a:b], T.wt[:, 4 * a:4 * b]).then_inc(qw[k], 1)

    if me is not None:
        V.wait_ge(S["lx"], nx)
        V.quantize_mx(T.xq[:, own:own + tw], T.xs[:, own:own + tw], T.xt[:, 0:4 * tw]).then_inc(qx, 1)
        pack(0)
        pack(1)
        if not owner[me]:
            pack(2)

    if me is not None:
        g.wait_ge(S["lgd"], 16)
        fused([(c, T["ge%d" % me][:, :], T.gd[:, :], S["ga"]) for c in gdest(me)])
        g.wait_ge(qx, 1)

        def src(plane, e, w):
            a = own + locate(P["xo"][me], me, run(e))
            return T.xs[:, a:a + w] if plane else codes("xq", a, a + w)

        def dst(plane, bufs, a, w):
            return T[bufs[1]][:, a:a + w] if plane else codes(bufs[0], a, a + w)

        def send_near(to):
            for e in grp[me]:
                w = size(me, run(e))
                if e != me and w and owner[e] == to:
                    for plane in (0, 1):
                        copy(cores[e], dst(plane, ("xq", "xs"), P["near"][e]["at"][me], w), src(plane, e, w), S["xin"], nearmask(me, e))

        def send_weights(a, b, ks, sem):
            for k in ks:
                g.wait_ge(qw[k], 1)
            copy(fx[me], codes("wq", a, b), codes("wq", a, b), sem)
            copy(fx[me], T.ws[:, a:b], T.ws[:, a:b], sem)

        fo = sorted([e for e in faro if size(me, run(e))], key=lambda e: (owner[e], e))
        for plane in (0, 1):
            for e in fo:
                w = P["fars"][e]["w"][me]
                if port[e] == core:
                    copy(fx[e], dst(plane, ("xq", "xs"), P["fars"][e]["at"][me], w), src(plane, e, w), S["fin"])
                else:
                    copy(port[e], dst(plane, ("rq", "rs"), rel[e]["at"][me], w), src(plane, e, w), S["relp" if plane else "relc"])
        if owner[me]:
            g.sem_inc(S["tok"], 1)
            send_near(True)
            send_near(False)
            pass_on()
        else:
            send_near(True)
            send_weights(0, 512, (0, 1), S["wa"])
            g.sem_inc(S["tok"], 1)
            send_near(False)
            send_weights(512, 640, (2,), S["wb"])
    else:
        home, there = grp[ex], far[ex]
        g.wait_ge(S["ga"], sum(share(cores[q], len(gdest(q)), core) for q in home))
        to = [e for k, e in enumerate(there) if k % 2 == hp[ex].index(core)]
        fused([(fx[e], T["ge%d" % q][:, :], T["ge%d" % q][:, :], S["gh"]) for e in to for q in home])
        pass_on()
    gb = [ev(), ev()]
    for u in units:
        a, b = cols[u]
        if b > a:
            g.wait_ge(S["lg%d" % u], ng[u])
            g.partition_broadcast(T.gb[:, a:b], T.gr[0:1, a:b], 128).then_inc(gb[u], 1)

    nxin = sum(2 * len(bits(nearmask(q, ex))) for q in nearq)
    nfin = sum(2 * engines(cores[q], core) for q in farq if cores[q] == port[ex]) + (2 * engines(port[ex], core) if rel[ex]["w"] else 0)
    if me is not None:
        arrived = [(qw[0], 1), (qw[1], 1), (qw[2], 1)]
    else:
        k = 2 * engines(cores[ex], core)
        arrived = [(S["wa"], k), (S["wa"], k), (S["wb"], k)]
    qhs, acts, done, zs, pz, weights = {}, {}, {}, {}, [ev(), ev()], [0]

    def product(bank, k, buf, lo, hi, sem):
        while weights[0] < min(k // 2 + 1, 3):
            M.wait_ge(*arrived[weights[0]])
            weights[0] += 1
        M.matmul_mx(T.z[:, 512 * bank:512 * bank + hi - lo], T.wq[:, 128 * k:128 * k + 128], T.ws[:, 128 * k:128 * k + 128],
                    T[buf[0]][:, lo:hi], T[buf[1]][:, lo:hi], True, True).then_inc(sem, 1)

    def make(i):
        lo, hi = spans[i]
        w, va, sa = hi - lo, ev(), ev()
        if i == 0:
            M.wait_ge(qx, 1)
            if nxin:
                M.wait_ge(S["xin"], nxin)
        elif nfin:
            M.wait_ge(S["fin"], nfin)
        for b in range(4):
            bank = 4 * i + b
            zs[i, b] = ev()
            product(bank, b, ("xq", "xs"), lo, hi, zs[i, b])
            E, z, o = (V, A)[b % 2], T.z[:, 512 * bank:512 * bank + w], T["h%d" % i][:, b:4 * w:4]
            E.wait_ge(zs[i, b], 1)
            if b % 2 == 0:
                V.tensor_scalar(o, z, 0.0, C, AluOpType.max, AluOpType.mult).then_inc(va, 1)
            else:
                A.activation(o, z, ActivationFunctionType.Relu, scale=C).then_inc(sa, 1)
        acts[i] = (va, sa)

    def quantise(i):
        w = spans[i][1] - spans[i][0]
        V.wait_ge(acts[i][0], 2)
        V.wait_ge(acts[i][1], 2)
        qhs[i] = ev()
        V.quantize_mx(T["hq%d" % i][:, 0:w], T["hs%d" % i][:, 0:w], T["h%d" % i][:, 0:4 * w]).then_inc(qhs[i], 1)

    def last(i):
        M.wait_ge(qhs[i], 1)
        product(4 * i, 4, ("hq%d" % i, "hs%d" % i), 0, spans[i][1] - spans[i][0], pz[i])

    def gated(i):
        a, b = cols[i]
        z0 = 512 * 4 * i + (f0 - nn if i else a0) - spans[i][0]
        ce, jobs = ev(), []
        if i == 0 and mine:
            r0 = locate(P["ro"][me][par], me, run(me))
            jobs.append((T["res%d" % par][:, r0:r0 + mine], 0, mine))
            a = mine
        if b > a:
            jobs.append((T.po[:, a:b], a, b))
        if jobs:
            V.wait_ge(gb[i], 1)
        V.wait_ge(pz[i], 1)
        for o, a, b in jobs:
            V.tensor_tensor(o, T.z[:, z0 + a:z0 + b], T.gb[:, a:b], AluOpType.mult).then_inc(ce, 1)
        done[i] = (ce, len(jobs))

    def leave(i):
        g.wait_ge(*done[i])
        for q, c, w in sorted(pieces[i], key=lambda t: -t[2]):
            if q != ex:
                a = locate(P["ro"][q][par], q, run(ex))
                copy(cores[q], T["res%d" % par][:, a:a + w], T.po[:, c:c + w], S["pl" if i else "pe"])

    if len(units) == 1:
        for step in (make, quantise, last, gated, leave):
            step(units[0])
    else:
        make(0)
        pack(2)
        make(1)
        for u in units:
            quantise(u)
            last(u)
        gated(0)
        gated(1)
        leave(0)
        leave(1)
    if me is None:
        g.wait_ge(S["ls"], local[0])
        return

    npe = sum(engines(cores[q], core) for q in grp[me] if q != me and size(me, run(q)))
    npl = sum(engines(fx[q], core) for q in faro if size(me, run(q)))
    adds = []
    for s in range(n):
        w = cnt[me][s]
        if not w:
            continue
        late = s in faro or (s + 1) % n in faro
        b0, b1 = [locate(P["ro"][me][p], me, [s]) for p in (0, 1)]
        if adds and adds[-1][0] == late and adds[-1][1] + adds[-1][4] == b0 and adds[-1][2] + adds[-1][4] == b1:
            adds[-1][4] += w
        else:
            adds.append([late, b0, b1, off[me][s], w])
    ys = ev()
    V.wait_ge(*done[0])
    if npe:
        V.wait_ge(S["pe"], npe)
    for late in (False, True):
        if late and npl:
            V.wait_ge(S["pl"], npl)
        for l, b0, b1, y0, w in adds:
            if l == late:
                V.tensor_tensor(T.ysb[:, y0:y0 + w], T.res0[:, b0:b0 + w], T.res1[:, b1:b1 + w], AluOpType.add).then_inc(ys, 1)
    Y.wait_ge(ys, len(adds))
    Y.dma_start(T.y[:, :], T.ysb[:, :]).then_inc(S["st"], 16)
    Y.wait_ge(S["st"], 16)
    g.wait_ge(S["ls"], local[0])
